import numpy as np
import ml_dtypes


def mxq(x, axis, fmt="e4m3"):
    dtype, down = {"e4m3": (ml_dtypes.float8_e4m3fn, 7), "e5m2": (ml_dtypes.float8_e5m2, 14)}[fmt]
    v = np.moveaxis(np.asarray(x, np.float32).astype(ml_dtypes.bfloat16).astype(np.float64), axis, -1)
    blocks = v.reshape(v.shape[:-1] + (-1, 32))
    amax = np.abs(blocks).max(-1, keepdims=True)
    byte = np.maximum(np.where(amax > 0, np.frexp(amax)[1] - 1 + 127, 0) - down, 1)
    scale = np.exp2(byte - 127.0)
    codes = (blocks / scale).astype(np.float32).astype(dtype).astype(np.float64)
    return np.moveaxis((codes * scale).reshape(v.shape), -1, axis)


WIDE = False


def mx_kscale(k):
    if not WIDE:
        return np.ones(k)
    levels = np.array([10, -10, 5, -5, 0])
    if k % 512:
        return np.exp2(np.random.permutation(np.resize(levels, k // 32))).repeat(32)
    a = np.empty((k // 512, 16))
    for p in range(k // 512):
        a[p, :8] = np.random.permutation(np.resize(levels, 8))
        for g in range(8):
            far = levels[np.abs(levels - a[p, g]) >= 10]
            a[p, g + 8] = far[np.random.randint(len(far))]
    return np.exp2(a.ravel()).repeat(32)


BF16 = ml_dtypes.bfloat16


def bf(x):
    return np.asarray(x, np.float32).astype(BF16)


def f64(x):
    return np.asarray(x).astype(np.float64)


E2M1 = np.array([0.0, 0.5, 1.0, 1.5, 2.0, 3.0, 4.0, 6.0, -0.0, -0.5, -1.0, -1.5, -2.0, -3.0, -4.0, -6.0])


def pack_weight(w, fmt):
    k, n = w.shape
    w = f64(bf(w)).reshape(k // 32, 32, n)
    amax = np.abs(w).max(1)
    if fmt == "e4m3":
        byte = np.frexp(amax)[1] - 1 + 127 - 7
    else:
        mant, ex = np.frexp(amax / 6.0)
        byte = np.where(mant > 0.5, ex, ex - 1) + 127
    byte = np.clip(np.where(amax > 0, byte, 1), 1, 254)
    scaled = (w * np.exp2(127.0 - byte)[:, None, :]).reshape(k, n).astype(np.float32)
    by_word = np.ascontiguousarray(scaled.reshape(k // 512, 128, 4, n).transpose(0, 1, 3, 2))
    if fmt == "e4m3":
        words = by_word.astype(ml_dtypes.float8_e4m3fn).view(np.uint8)
    else:
        c = by_word.astype(ml_dtypes.float4_e2m1fn).view(np.uint8) & 0xF
        words = c[..., 0::2] | (c[..., 1::2] << 4)
    return np.ascontiguousarray(words), np.ascontiguousarray(byte.astype(np.uint8).reshape(k // 512, 16, n))


def unpack_weight(words, scales, fmt):
    g, p, n, _ = words.shape
    if fmt == "e4m3":
        vals = np.ascontiguousarray(words).view(ml_dtypes.float8_e4m3fn).astype(np.float64)
    else:
        nib = np.empty((g, p, n, 4), np.uint8)
        nib[..., 0::2] = words & 0xF
        nib[..., 1::2] = words >> 4
        vals = E2M1[nib]
    vals = vals * np.repeat(np.exp2(scales.astype(np.float64) - 127.0), 8, axis=1)[..., None]
    return vals.transpose(0, 1, 3, 2).reshape(g * 512, n)
def pack4(w):
    words, scales = pack_weight(w, "e2m1")
    return words.reshape(words.shape[0], 128, -1), scales


def unpack4(words, scales):
    return unpack_weight(words.reshape(words.shape[0], 128, -1, 2), scales, "e2m1")


R, V, K, C = 1024, 1536, 2048, 512


def setup_inputs():
    s, u = mx_kscale(V), mx_kscale(K)
    t = mx_kscale(R)
    x = np.random.randint(0, 2, (R, V)).astype(np.float64)
    j = np.random.standard_normal((V, V))
    j = (j + j.T) / np.sqrt(V)
    np.fill_diagonal(j, 0.0)
    beta = np.random.uniform(0.5, 3.0, (R, 1))
    sw, ss = pack4(x.T * s[:, None])
    cw, cs = pack4(j / s[:, None])
    return {"states_words": sw, "states_scales": ss,
            "couplings_words": cw, "couplings_scales": cs,
            "flip": bf((2.0 * x - 1.0) * beta),
            "weight": bf(np.random.uniform(0.5, 1.5, R) * t),
            "traces": bf(np.random.standard_normal((R, K)) * u / t[:, None]),
            "proj": bf(np.random.standard_normal((K, C)) / np.sqrt(K) / R ** 0.25 / u[:, None])}


def reference(states_words, states_scales, couplings_words, couplings_scales, flip, weight, traces, proj):
    x = unpack4(states_words, states_scales)
    j = unpack4(couplings_words, couplings_scales)
    field = x.T @ j
    gain = field * f64(flip)
    prob = 1.0 / (1.0 + np.exp(-gain))
    a = prob * f64(weight)[:, None]
    z = mxq(f64(traces), 1, "e4m3") @ mxq(f64(proj), 0, "e4m3")
    return mxq(a, 0, "e4m3").T @ mxq(z, 0, "e4m3")

@@ -1,0 +1,355 @@
+from contextlib import ExitStack
+
+import concourse.mybir as mybir
+from concourse.masks import make_identity
+
+R, V, K, C = 1024, 1536, 2048, 512
+FLOPS = 2 * R * V * V + 2 * R * K * C + 2 * R * V * C
+
+F32 = mybir.dt.float32
+BF16 = mybir.dt.bfloat16
+I32 = mybir.dt.int32
+U32 = mybir.dt.uint32
+U8 = mybir.dt.uint8
+FP8X4 = mybir.dt.float8_e4m3fn_x4
+FP4X4 = mybir.dt.float4_e2m1fn_x4
+ACT = mybir.ActivationFunctionType
+ALU = mybir.AluOpType
+
+P = 128
+SLOTS = 4
+PASS = P * SLOTS
+BANK = 512
+BANKS = 8
+RUN = 4
+R_PASSES = R // PASS
+V_PASSES = V // PASS
+K_PASSES = K // PASS
+V_CHUNKS = V // BANK
+QUADS = 4
+
+
+def tile_qubo_replica_flips_s12_kernel(
+    tc, states_words, states_scales, couplings_words, couplings_scales, flip, weight, traces, proj, out
+):
+    nc = tc.nc
+    with ExitStack() as ctx:
+        keep = ctx.enter_context(tc.tile_pool(name="keep", bufs=1))
+        work = ctx.enter_context(tc.tile_pool(name="work", bufs=4))
+        psum = ctx.enter_context(tc.psum_pool(name="psum", bufs=1))
+        ctx.enter_context(tc.manual_schedule())
+
+        banks_used = []
+
+        def bank_tile(shape):
+            tag = "bank%d" % (len(banks_used) % BANKS)
+            banks_used.append(tag)
+            return psum.tile(shape, F32, name=tag, tag=tag)
+
+        def kept(name, shape, dtype):
+            return keep.tile(shape, dtype, name=name, tag=name, align_bytes=64)
+
+        def wide_tile(shape, dtype):
+            return work.tile(shape, dtype, name="wide", tag="wide", bufs=V_CHUNKS, align_bytes=64)
+
+        def mx_pair(name):
+            return kept(name + "_codes", [P, BANK], U32), kept(name + "_scales", [P, BANK], U8)
+
+        def grouped_tile(tag, bufs):
+            return work.tile([P, BANK, SLOTS], BF16, name=tag, tag=tag, bufs=bufs, align_bytes=64)
+
+        def quantize(pair, grouped, c0=0, c1=BANK):
+            codes, scales = pair
+            nc.vector.quantize_mx(
+                out=codes[:, c0:c1].bitcast(FP8X4),
+                scales=scales[:, c0:c1],
+                in_=grouped[:, c0:c1, :].rearrange("p c t -> p (c t)"),
+            )
+
+        def interleave(copy, grouped, rows, c0=0, c1=BANK):
+            copy(
+                out=grouped[:, c0:c1, :].rearrange("p (c i) t -> p c t i", i=4),
+                in_=rows[:, :, c0:c1].rearrange("p t (c i) -> p c t i", i=4),
+            )
+
+        x_raw = [kept("x_raw%d" % g, [P, V_PASSES, PASS // 2], I32) for g in range(R_PASSES)]
+        xs_raw = kept("xs_raw", [P, V_PASSES, R // 4], I32)
+        j_words = [kept("j_words%d" % c, [P, V_PASSES, 2 * BANK], U8) for c in range(V_CHUNKS)]
+        j_scales = kept("j_scales", [P, V_PASSES, V], U8)
+        flip_sb = [
+            [kept("flip%d_%d" % (c, g), [P, SLOTS, BANK], BF16) for g in range(R_PASSES)] for c in range(V_CHUNKS)
+        ]
+        tr_pieces = [(0, 0, 1), (0, 1, 1), (0, 2, 2), (1, 0, 2), (1, 2, 2)]
+        tr_raw = {}
+        for g, kp, n in tr_pieces:
+            shape = [P, RUN, n * PASS]
+            piece = wide_tile(shape, BF16) if n == 2 else kept("tr_first%d" % kp, shape, BF16)
+            for j in range(n):
+                tr_raw[(g, kp + j)] = (piece, j)
+        proj_raw = [kept("proj_raw%d" % kp, [P, SLOTS, C], BF16) for kp in range(K_PASSES)]
+        w_rows = kept("w_rows", [SLOTS, R_PASSES * P], BF16)
+        w_wide = kept("w_wide", [P, R_PASSES * P], F32)
+        w_col = kept("w_col", [P, R_PASSES, SLOTS], F32)
+        ident = kept("ident", [P, P], F32)
+        warm = kept("warm", [P, 1], F32)
+
+        x_codes = [kept("x_codes%d" % g, [P, V_PASSES, SLOTS, 2 * P], U8) for g in range(R_PASSES)]
+        x_scales = [kept("x_scales%d" % g, [P, V_PASSES, SLOTS, P], U8) for g in range(R_PASSES)]
+        proj_q = [mx_pair("proj_q%d" % kp) for kp in range(K_PASSES)]
+        tr_q = [[mx_pair("tr_q%d_%d" % (g, kp)) for kp in range(K_PASSES)] for g in range(R_PASSES)]
+        z_q = [mx_pair("z_q%d" % g) for g in range(R_PASSES)]
+        a_q = [[mx_pair("a_q%d_%d" % (c, g)) for g in range(R_PASSES)] for c in range(V_CHUNKS)]
+
+        def load_x_words(g):
+            src = states_words.bitcast(I32)[:, :, g * PASS // 2 : (g + 1) * PASS // 2]
+            nc.sync.dma_start(out=x_raw[g][:], in_=src.rearrange("k p n -> p k n"))
+
+        def load_j_words(c):
+            src = couplings_words.bitcast(I32)[:, :, c * BANK // 2 : (c + 1) * BANK // 2]
+            nc.sync.dma_start(out=j_words[c][:].bitcast(I32), in_=src.rearrange("k p n -> p k n"))
+
+        def load_scale_rows(plane, scales, quads):
+            src = scales.bitcast(I32)
+            for q in quads:
+                nc.sync.dma_start(
+                    out=plane[32 * q : 32 * q + 4, :, :],
+                    in_=src[:, 4 * q : 4 * q + 4, :].rearrange("k r n -> r k n"),
+                )
+
+        def load_flip(c, g):
+            src = flip[g * PASS : (g + 1) * PASS, c * BANK : (c + 1) * BANK]
+            src = src.rearrange("(m t i) v -> i m t v", t=SLOTS, i=RUN)
+            for i in range(RUN):
+                nc.sync.dma_start(out=flip_sb[c][g][i:P:RUN, :, :], in_=src[i])
+
+        def load_traces(g, kp):
+            piece = tr_raw[(g, kp)][0]
+            src = traces[g * PASS : (g + 1) * PASS, kp * PASS : kp * PASS + piece.shape[2]]
+            nc.sync.dma_start(out=piece[:], in_=src.rearrange("(a i) k -> a i k", i=RUN))
+
+        def load_proj(kp):
+            src = proj[kp * PASS : (kp + 1) * PASS, :]
+            nc.sync.dma_start(out=proj_raw[kp][:], in_=src.rearrange("(p t) c -> p t c", t=SLOTS))
+
+        js_words = j_scales[:].bitcast(I32)
+        nc.vector.memset(xs_raw[:], 0)
+        nc.vector.memset(js_words, 0)
+        nc.vector.memset(warm[:], 0.0)
+        nc.scalar.activation(out=warm[:], in_=warm[:], func=ACT.Sigmoid)
+        make_identity(nc, ident[:])
+        nc.gpsimd.memset(w_wide[:], 0.0)
+
+        load_traces(0, 0)
+        load_scale_rows(xs_raw, states_scales, range(QUADS))
+        load_x_words(0)
+        load_j_words(0)
+        load_scale_rows(js_words, couplings_scales, range(QUADS))
+        load_flip(0, 0)
+        load_traces(0, 1)
+        load_x_words(1)
+        nc.sync.dma_start(
+            out=w_rows[:].rearrange("t (a i) -> t a i", i=RUN),
+            in_=weight.rearrange("(a t i) -> t a i", t=SLOTS, i=RUN),
+        )
+        nc.gpsimd.tensor_copy(out=w_wide[0:SLOTS, :], in_=w_rows[:])
+        load_proj(0)
+        load_flip(0, 1)
+        load_traces(0, 2)
+        load_proj(1)
+        load_j_words(1)
+        load_flip(1, 0)
+        load_proj(2)
+        load_flip(1, 1)
+        load_proj(3)
+        load_traces(1, 0)
+        load_traces(1, 2)
+        load_j_words(2)
+        load_flip(2, 0)
+        load_flip(2, 1)
+
+        def order_states(g):
+            nc.vector.tensor_copy(
+                out=x_scales[g][:].bitcast(I32),
+                in_=xs_raw[:].rearrange("p k (g m t) -> p g k t m", g=R_PASSES, t=SLOTS)[:, g],
+            )
+            for t in range(SLOTS):
+                nc.vector.tensor_copy(
+                    out=x_codes[g][:, :, t, :].bitcast(I32).rearrange("p k (m h) -> p k m h", h=2),
+                    in_=x_raw[g][:].rearrange("p k (m t h) -> p t k m h", t=SLOTS, h=2)[:, t],
+                )
+
+        prob = {}
+
+        def field_step(c, g, t):
+            bank = bank_tile([P, BANK])
+            for k in range(V_PASSES):
+                nc.tensor.matmul_mx(
+                    out=bank[:],
+                    lhsT=x_codes[g][:, k, t, :].bitcast(FP4X4),
+                    lhsT_scale=x_scales[g][:, k, t, :],
+                    rhs=j_words[c][:, k, :].bitcast(FP4X4),
+                    rhs_scale=j_scales[:, k, c * BANK : (c + 1) * BANK],
+                    start=(k == 0),
+                    stop=(k == V_PASSES - 1),
+                )
+            pr = work.tile([P, BANK], F32, name="prob", tag="prob", bufs=16)
+            nc.vector.tensor_tensor(out=pr[:], in0=bank[:], in1=flip_sb[c][g][:, t, :], op=ALU.mult)
+            nc.scalar.activation(out=pr[:], in_=pr[:], func=ACT.Sigmoid)
+            prob[(c, g, t)] = pr
+
+        tr_grouped = {}
+
+        def turn_step(g, kp, e):
+            if e == 0:
+                tr_grouped[(g, kp)] = grouped_tile("tr_grouped", 3)
+            piece, j = tr_raw[(g, kp)]
+            words = piece[:].bitcast(F32)
+            w0 = j * (PASS // 2)
+            bank = bank_tile([P, 2, 2, P])
+            for x in range(2):
+                for u in range(2):
+                    nc.tensor.transpose(
+                        bank[:, x, u, :], words[:, 2 * e + x, w0 + u : w0 + PASS // 2 : 2], ident[:]
+                    )
+            dst = tr_grouped[(g, kp)][:].rearrange("p c t -> p (c t)").bitcast(F32)
+            nc.scalar.copy(
+                out=dst.rearrange("p (t m e w) -> p e m t w", t=SLOTS, e=2, w=4)[:, e],
+                in_=bank[:].rearrange("p x u (m t) -> p m t (x u)", t=SLOTS),
+            )
+
+        def weight_step():
+            bank = bank_tile([P, R_PASSES, P])
+            for g in range(R_PASSES):
+                nc.tensor.transpose(bank[:, g, :], w_wide[:, g * P : (g + 1) * P], ident[:])
+            nc.scalar.copy(out=w_col[:], in_=bank[:, :, 0:SLOTS])
+
+        z_grouped = {}
+
+        def descriptor_step(g, cq):
+            if cq == 0:
+                z_grouped[g] = grouped_tile("z_grouped", 1)
+            cols = slice(cq * P, (cq + 1) * P)
+            bank = bank_tile([P, SLOTS, P])
+            for t in range(SLOTS):
+                reps = slice(t * P, (t + 1) * P)
+                for kp in range(K_PASSES):
+                    nc.tensor.matmul_mx(
+                        out=bank[:, t, :],
+                        lhsT=tr_q[g][kp][0][:, reps].bitcast(FP8X4),
+                        lhsT_scale=tr_q[g][kp][1][:, reps],
+                        rhs=proj_q[kp][0][:, cols].bitcast(FP8X4),
+                        rhs_scale=proj_q[kp][1][:, cols],
+                        start=(kp == 0),
+                        stop=(kp == K_PASSES - 1),
+                    )
+            nc.scalar.copy(out=z_grouped[g][:, cols, :], in_=bank[:].rearrange("p t c -> p c t"))
+
+        results = {}
+
+        def out_step(c, j, copy):
+            cols = slice(j * P, (j + 1) * P)
+            bank = bank_tile([P, C])
+            for g in range(R_PASSES):
+                nc.tensor.matmul_mx(
+                    out=bank[:],
+                    lhsT=a_q[c][g][0][:, cols].bitcast(FP8X4),
+                    lhsT_scale=a_q[c][g][1][:, cols],
+                    rhs=z_q[g][0][:].bitcast(FP8X4),
+                    rhs_scale=z_q[g][1][:],
+                    start=(g == 0),
+                    stop=(g == R_PASSES - 1),
+                )
+            if j == 0:
+                results[c] = wide_tile([P, BANK // P, C], F32)
+            copy(out=results[c][:, j, :], in_=bank[:])
+            nc.sync.dma_start(out=out[c * BANK + j * P : c * BANK + (j + 1) * P, :], in_=results[c][:, j, :])
+
+        proj_grouped = {}
+
+        def proj_interleave(kp, copy):
+            proj_grouped[kp] = grouped_tile("grouped", 3)
+            interleave(copy, proj_grouped[kp], proj_raw[kp])
+
+        a_rows = {}
+        a_grouped = {}
+
+        def weigh(c, g, t, on_scalar):
+            if t == 0:
+                a_rows[(c, g)] = work.tile([P, SLOTS, BANK], BF16, name="a_rows", tag="a_rows", bufs=2)
+            dst = a_rows[(c, g)][:, t, :]
+            if on_scalar:
+                nc.scalar.activation(out=dst, in_=prob[(c, g, t)][:], func=ACT.Copy, scale=w_col[:, g, t : t + 1])
+            else:
+                nc.vector.tensor_scalar(
+                    out=dst, in0=prob[(c, g, t)][:], scalar1=w_col[:, g, t : t + 1], scalar2=None, op0=ALU.mult
+                )
+
+        def a_interleave(c, g, c0, c1):
+            if c0 == 0:
+                a_grouped[(c, g)] = grouped_tile("grouped", 3)
+            interleave(nc.vector.tensor_copy, a_grouped[(c, g)], a_rows[(c, g)], c0, c1)
+
+        def fields(c, g):
+            return [lambda t=t: field_step(c, g, t) for t in range(SLOTS)]
+
+        def turns(g, kps):
+            return [lambda kp=kp, e=e: turn_step(g, kp, e) for kp in kps for e in range(2)]
+
+        def descriptors(g):
+            return [lambda cq=cq: descriptor_step(g, cq) for cq in range(C // P)]
+
+        def outs(c, js, copy=nc.scalar.copy):
+            return [lambda j=j: out_step(c, j, copy) for j in js]
+
+        def weighs(c, g, on_scalar=False):
+            return [lambda t=t: weigh(c, g, t, on_scalar) for t in range(SLOTS)]
+
+        def a_il(c, g, c0=0, c1=BANK):
+            return lambda: a_interleave(c, g, c0, c1)
+
+        def a_qz(c, g, c0=0, c1=BANK):
+            return lambda: quantize(a_q[c][g], a_grouped[(c, g)], c0, c1)
+
+        def tr_qz(g, kp):
+            return lambda: quantize(tr_q[g][kp], tr_grouped[(g, kp)])
+
+        def pj_il(kp, copy=nc.vector.tensor_copy):
+            return lambda: proj_interleave(kp, copy)
+
+        def pj_qz(kp):
+            return lambda: quantize(proj_q[kp], proj_grouped[kp])
+
+        def z_qz(g):
+            return lambda: quantize(z_q[g], z_grouped[g])
+
+        def phase(steps, after):
+            for step, side in zip(steps, after):
+                step()
+                for task in side:
+                    task()
+
+        half = BANK // 2
+        phase(turns(0, [0]), [[], [lambda: order_states(0), tr_qz(0, 0)]])
+        phase(fields(0, 0), [[], [], [], [lambda: order_states(1)]])
+        phase(turns(0, [1]), [[], [pj_il(0)]])
+        weight_step()
+        w00 = weighs(0, 0, True)
+        phase(fields(0, 1), [[pj_qz(0), w00[0]], [tr_qz(0, 1), w00[1]], [w00[2]], [w00[3], pj_il(1)]])
+        phase(turns(0, [2, 3]), [[], [pj_qz(1)], [], []])
+        w01 = weighs(0, 1, True)
+        phase(fields(1, 0), [[tr_qz(0, 2), w01[0]], [tr_qz(0, 3), pj_il(2), w01[1]], [w01[2]], [pj_qz(2), w01[3]]])
+        phase(fields(1, 1), [[pj_il(3)], [pj_qz(3)], [], [a_il(0, 0)]])
+        phase(turns(1, [0, 1]), [[], [a_il(0, 1), a_qz(0, 0)], [tr_qz(1, 0)], [a_qz(0, 1), tr_qz(1, 1)]])
+        phase(descriptors(0)[:2], [weighs(1, 0), [a_il(1, 0)]])
+        phase(turns(1, [2, 3]), [[a_qz(1, 0)], [], [tr_qz(1, 2)], [tr_qz(1, 3)]])
+        phase(descriptors(0)[2:], [[], weighs(1, 1, True)])
+        phase(fields(2, 0), [[z_qz(0)], [], [], [a_il(1, 1)]])
+        phase(descriptors(1), [weighs(2, 0) + [a_qz(1, 1)], [a_il(2, 0)], [], [a_qz(2, 0)]])
+        last = weighs(2, 1)
+        phase(fields(2, 1)[:3], [[z_qz(1)], last[:1], last[1:2]])
+        phase(outs(0, range(2)), [[], []])
+        phase(fields(2, 1)[3:], [last[2:]])
+        phase(outs(0, range(2, 4)), [[a_il(2, 1, 0, half), a_il(2, 1, half, BANK)], [a_qz(2, 1, 0, half)]])
+        phase(outs(1, range(4)), [[a_qz(2, 1, half, BANK)], [], [], []])
+        for j in range(4):
+            out_step(2, j, nc.vector.tensor_copy if j % 2 else nc.scalar.copy)

@@ -21,12 +21,12 @@ SLOTS = 4
 PASS = P * SLOTS
 BANK = 512
 BANKS = 8
-RUN = 4
 R_PASSES = R // PASS
 V_PASSES = V // PASS
 K_PASSES = K // PASS
 V_CHUNKS = V // BANK
 QUADS = 4
+PROJ_SPLIT = 256
 
 
 def tile_qubo_replica_flips_s12_kernel(
@@ -72,24 +72,22 @@ def tile_qubo_replica_flips_s12_kernel(
                 in_=rows[:, :, c0:c1].rearrange("p t (c i) -> p c t i", i=4),
             )
 
-        x_raw = [kept("x_raw%d" % g, [P, V_PASSES, PASS // 2], I32) for g in range(R_PASSES)]
-        xs_raw = kept("xs_raw", [P, V_PASSES, R // 4], I32)
+        x_raw = [kept("x_raw%d" % g, [P, V_PASSES, 2 * PASS], U8) for g in range(R_PASSES)]
+        xs_raw = kept("xs_raw", [P, V_PASSES, R], U8)
         j_words = [kept("j_words%d" % c, [P, V_PASSES, 2 * BANK], U8) for c in range(V_CHUNKS)]
-        j_scales = kept("j_scales", [P, V_PASSES, V], U8)
+        j_scales = [kept("j_scales%d" % n, [P, V_PASSES, w], U8) for n, w in enumerate((BANK, V - BANK))]
         flip_sb = [
             [kept("flip%d_%d" % (c, g), [P, SLOTS, BANK], BF16) for g in range(R_PASSES)] for c in range(V_CHUNKS)
         ]
         tr_pieces = [(0, 0, 1), (0, 1, 1), (0, 2, 2), (1, 0, 2), (1, 2, 2)]
         tr_raw = {}
         for g, kp, n in tr_pieces:
-            shape = [P, RUN, n * PASS]
+            shape = [P, SLOTS, n * PASS]
             piece = wide_tile(shape, BF16) if n == 2 else kept("tr_first%d" % kp, shape, BF16)
             for j in range(n):
                 tr_raw[(g, kp + j)] = (piece, j)
         proj_raw = [kept("proj_raw%d" % kp, [P, SLOTS, C], BF16) for kp in range(K_PASSES)]
-        w_rows = kept("w_rows", [SLOTS, R_PASSES * P], BF16)
-        w_wide = kept("w_wide", [P, R_PASSES * P], F32)
-        w_col = kept("w_col", [P, R_PASSES, SLOTS], F32)
+        w_raw = kept("w_raw", [P, R_PASSES, SLOTS], BF16)
         ident = kept("ident", [P, P], F32)
         warm = kept("warm", [P, 1], F32)
 
@@ -102,81 +100,77 @@ def tile_qubo_replica_flips_s12_kernel(
 
         def load_x_words(g):
             src = states_words.bitcast(I32)[:, :, g * PASS // 2 : (g + 1) * PASS // 2]
-            nc.sync.dma_start(out=x_raw[g][:], in_=src.rearrange("k p n -> p k n"))
+            nc.sync.dma_start(out=x_raw[g][:].bitcast(I32), in_=src.rearrange("k p n -> p k n"))
 
         def load_j_words(c):
             src = couplings_words.bitcast(I32)[:, :, c * BANK // 2 : (c + 1) * BANK // 2]
             nc.sync.dma_start(out=j_words[c][:].bitcast(I32), in_=src.rearrange("k p n -> p k n"))
 
-        def load_scale_rows(plane, scales, quads):
-            src = scales.bitcast(I32)
-            for q in quads:
-                nc.sync.dma_start(
+        def load_scale_rows(queue, plane, scales, a, b):
+            src = scales.bitcast(I32)[:, :, a // 4 : b // 4]
+            for q in range(QUADS):
+                queue.dma_start(
                     out=plane[32 * q : 32 * q + 4, :, :],
                     in_=src[:, 4 * q : 4 * q + 4, :].rearrange("k r n -> r k n"),
                 )
 
         def load_flip(c, g):
             src = flip[g * PASS : (g + 1) * PASS, c * BANK : (c + 1) * BANK]
-            src = src.rearrange("(m t i) v -> i m t v", t=SLOTS, i=RUN)
-            for i in range(RUN):
-                nc.sync.dma_start(out=flip_sb[c][g][i:P:RUN, :, :], in_=src[i])
+            nc.sync.dma_start(out=flip_sb[c][g][:], in_=src.rearrange("(p t) v -> p t v", t=SLOTS))
 
         def load_traces(g, kp):
             piece = tr_raw[(g, kp)][0]
             src = traces[g * PASS : (g + 1) * PASS, kp * PASS : kp * PASS + piece.shape[2]]
-            nc.sync.dma_start(out=piece[:], in_=src.rearrange("(a i) k -> a i k", i=RUN))
+            nc.sync.dma_start(out=piece[:], in_=src.rearrange("(p t) k -> p t k", t=SLOTS))
 
         def load_proj(kp):
             src = proj[kp * PASS : (kp + 1) * PASS, :]
             nc.sync.dma_start(out=proj_raw[kp][:], in_=src.rearrange("(p t) c -> p t c", t=SLOTS))
 
-        js_words = j_scales[:].bitcast(I32)
-        nc.vector.memset(xs_raw[:], 0)
-        nc.vector.memset(js_words, 0)
+        xs_words = xs_raw[:].bitcast(I32)
+        js_words = [plane[:].bitcast(I32) for plane in j_scales]
+        nc.vector.memset(xs_words, 0)
+        nc.vector.memset(js_words[0], 0)
+        nc.vector.memset(js_words[1], 0)
         nc.vector.memset(warm[:], 0.0)
         nc.scalar.activation(out=warm[:], in_=warm[:], func=ACT.Sigmoid)
         make_identity(nc, ident[:])
-        nc.gpsimd.memset(w_wide[:], 0.0)
 
         load_traces(0, 0)
-        load_scale_rows(xs_raw, states_scales, range(QUADS))
+        load_scale_rows(nc.sync, xs_words, states_scales, 0, R)
         load_x_words(0)
         load_j_words(0)
-        load_scale_rows(js_words, couplings_scales, range(QUADS))
+        load_scale_rows(nc.sync, js_words[0], couplings_scales, 0, BANK)
+        load_scale_rows(nc.gpsimd, js_words[1], couplings_scales, BANK, V)
         load_flip(0, 0)
-        load_traces(0, 1)
         load_x_words(1)
-        nc.sync.dma_start(
-            out=w_rows[:].rearrange("t (a i) -> t a i", i=RUN),
-            in_=weight.rearrange("(a t i) -> t a i", t=SLOTS, i=RUN),
-        )
-        nc.gpsimd.tensor_copy(out=w_wide[0:SLOTS, :], in_=w_rows[:])
+        load_traces(0, 1)
+        nc.sync.dma_start(out=w_raw[:], in_=weight.rearrange("(g p t) -> p g t", g=R_PASSES, t=SLOTS))
         load_proj(0)
         load_flip(0, 1)
         load_traces(0, 2)
-        load_proj(1)
         load_j_words(1)
+        load_proj(1)
         load_flip(1, 0)
         load_proj(2)
         load_flip(1, 1)
-        load_proj(3)
         load_traces(1, 0)
-        load_traces(1, 2)
         load_j_words(2)
+        load_proj(3)
         load_flip(2, 0)
+        load_traces(1, 2)
         load_flip(2, 1)
 
-        def order_states(g):
+        def order_scales(g):
             nc.vector.tensor_copy(
-                out=x_scales[g][:].bitcast(I32),
-                in_=xs_raw[:].rearrange("p k (g m t) -> p g k t m", g=R_PASSES, t=SLOTS)[:, g],
+                out=x_scales[g][:], in_=xs_raw[:].rearrange("p k (g m t) -> p g k t m", g=R_PASSES, t=SLOTS)[:, g]
             )
-            for t in range(SLOTS):
-                nc.vector.tensor_copy(
-                    out=x_codes[g][:, :, t, :].bitcast(I32).rearrange("p k (m h) -> p k m h", h=2),
-                    in_=x_raw[g][:].rearrange("p k (m t h) -> p t k m h", t=SLOTS, h=2)[:, t],
-                )
+
+        def order_words(g, t):
+            nc.vector.tensor_copy(
+                out=x_codes[g][:, :, t, :].rearrange("p k (m h) -> p k m h", h=2),
+                in_=x_raw[g][:].rearrange("p k (m t h) -> p t k m h", t=SLOTS, h=2)[:, t],
+            )
 
         prob = {}
 
@@ -188,11 +182,11 @@ def tile_qubo_replica_flips_s12_kernel(
                     lhsT=x_codes[g][:, k, t, :].bitcast(FP4X4),
                     lhsT_scale=x_scales[g][:, k, t, :],
                     rhs=j_words[c][:, k, :].bitcast(FP4X4),
-                    rhs_scale=j_scales[:, k, c * BANK : (c + 1) * BANK],
+                    rhs_scale=j_scales[0][:, k, :] if c == 0 else j_scales[1][:, k, (c - 1) * BANK : c * BANK],
                     start=(k == 0),
                     stop=(k == V_PASSES - 1),
                 )
-            pr = work.tile([P, BANK], F32, name="prob", tag="prob", bufs=16)
+            pr = work.tile([P, BANK], F32, name="prob", tag="prob", bufs=11)
             nc.vector.tensor_tensor(out=pr[:], in0=bank[:], in1=flip_sb[c][g][:, t, :], op=ALU.mult)
             nc.scalar.activation(out=pr[:], in_=pr[:], func=ACT.Sigmoid)
             prob[(c, g, t)] = pr
@@ -213,21 +207,15 @@ def tile_qubo_replica_flips_s12_kernel(
                     )
             dst = tr_grouped[(g, kp)][:].rearrange("p c t -> p (c t)").bitcast(F32)
             nc.scalar.copy(
-                out=dst.rearrange("p (t m e w) -> p e m t w", t=SLOTS, e=2, w=4)[:, e],
-                in_=bank[:].rearrange("p x u (m t) -> p m t (x u)", t=SLOTS),
+                out=dst.rearrange("p (e x m u) -> p e x m u", e=2, x=2, u=2)[:, e],
+                in_=bank[:].rearrange("p x u m -> p x m u"),
             )
-
-        def weight_step():
-            bank = bank_tile([P, R_PASSES, P])
-            for g in range(R_PASSES):
-                nc.tensor.transpose(bank[:, g, :], w_wide[:, g * P : (g + 1) * P], ident[:])
-            nc.scalar.copy(out=w_col[:], in_=bank[:, :, 0:SLOTS])
 
         z_grouped = {}
 
         def descriptor_step(g, cq):
             if cq == 0:
-                z_grouped[g] = grouped_tile("z_grouped", 1)
+                z_grouped[g] = grouped_tile("z_grouped", 2)
             cols = slice(cq * P, (cq + 1) * P)
             bank = bank_tile([P, SLOTS, P])
             for t in range(SLOTS):
@@ -266,22 +254,39 @@ def tile_qubo_replica_flips_s12_kernel(
 
         proj_grouped = {}
 
-        def proj_interleave(kp, copy):
+        def proj_interleave(kp):
             proj_grouped[kp] = grouped_tile("grouped", 3)
-            interleave(copy, proj_grouped[kp], proj_raw[kp])
+            interleave(nc.vector.tensor_copy, proj_grouped[kp], proj_raw[kp], 0, PROJ_SPLIT)
+            interleave(nc.scalar.copy, proj_grouped[kp], proj_raw[kp], PROJ_SPLIT, C)
 
         a_rows = {}
         a_grouped = {}
 
-        def weigh(c, g, t, on_scalar):
+        def a_rows_tile(c, g):
+            a_rows[(c, g)] = work.tile([P, SLOTS, BANK], BF16, name="a_rows", tag="a_rows", bufs=4)
+
+        def weigh_on_vector(c, g, t):
             if t == 0:
-                a_rows[(c, g)] = work.tile([P, SLOTS, BANK], BF16, name="a_rows", tag="a_rows", bufs=2)
-            dst = a_rows[(c, g)][:, t, :]
-            if on_scalar:
-                nc.scalar.activation(out=dst, in_=prob[(c, g, t)][:], func=ACT.Copy, scale=w_col[:, g, t : t + 1])
-            else:
-                nc.vector.tensor_scalar(
-                    out=dst, in0=prob[(c, g, t)][:], scalar1=w_col[:, g, t : t + 1], scalar2=None, op0=ALU.mult
+                a_rows_tile(c, g)
+            nc.vector.tensor_scalar(
+                out=a_rows[(c, g)][:, t, :],
+                in0=prob[(c, g, t)][:],
+                scalar1=w_raw[:, g, t : t + 1],
+                scalar2=None,
+                op0=ALU.mult,
+            )
+
+        def weigh_on_gpsimd(c, g, slots):
+            w_col = kept("w_col%d_%d" % (c, g), [P, SLOTS], F32)
+            nc.vector.tensor_copy(out=w_col[:], in_=w_raw[:, g, :])
+            for t in slots:
+                nc.gpsimd.tensor_scalar(
+                    out=a_rows[(c, g)][:, t, :],
+                    in0=prob[(c, g, t)][:],
+                    scalar1=w_col[:, t : t + 1],
+                    scalar2=0.0,
+                    op0=ALU.mult,
+                    op1=ALU.add,
                 )
 
         def a_interleave(c, g, c0, c1):
@@ -301,8 +306,8 @@ def tile_qubo_replica_flips_s12_kernel(
         def outs(c, js, copy=nc.scalar.copy):
             return [lambda j=j: out_step(c, j, copy) for j in js]
 
-        def weighs(c, g, on_scalar=False):
-            return [lambda t=t: weigh(c, g, t, on_scalar) for t in range(SLOTS)]
+        def weighs(c, g):
+            return [lambda t=t: weigh_on_vector(c, g, t) for t in range(SLOTS)]
 
         def a_il(c, g, c0=0, c1=BANK):
             return lambda: a_interleave(c, g, c0, c1)
@@ -313,8 +318,8 @@ def tile_qubo_replica_flips_s12_kernel(
         def tr_qz(g, kp):
             return lambda: quantize(tr_q[g][kp], tr_grouped[(g, kp)])
 
-        def pj_il(kp, copy=nc.vector.tensor_copy):
-            return lambda: proj_interleave(kp, copy)
+        def pj_il(kp):
+            return lambda: proj_interleave(kp)
 
         def pj_qz(kp):
             return lambda: quantize(proj_q[kp], proj_grouped[kp])
@@ -329,27 +334,35 @@ def tile_qubo_replica_flips_s12_kernel(
                     task()
 
         half = BANK // 2
-        phase(turns(0, [0]), [[], [lambda: order_states(0), tr_qz(0, 0)]])
-        phase(fields(0, 0), [[], [], [], [lambda: order_states(1)]])
-        phase(turns(0, [1]), [[], [pj_il(0)]])
-        weight_step()
-        w00 = weighs(0, 0, True)
-        phase(fields(0, 1), [[pj_qz(0), w00[0]], [tr_qz(0, 1), w00[1]], [w00[2]], [w00[3], pj_il(1)]])
-        phase(turns(0, [2, 3]), [[], [pj_qz(1)], [], []])
-        w01 = weighs(0, 1, True)
-        phase(fields(1, 0), [[tr_qz(0, 2), w01[0]], [tr_qz(0, 3), pj_il(2), w01[1]], [w01[2]], [pj_qz(2), w01[3]]])
-        phase(fields(1, 1), [[pj_il(3)], [pj_qz(3)], [], [a_il(0, 0)]])
-        phase(turns(1, [0, 1]), [[], [a_il(0, 1), a_qz(0, 0)], [tr_qz(1, 0)], [a_qz(0, 1), tr_qz(1, 1)]])
-        phase(descriptors(0)[:2], [weighs(1, 0), [a_il(1, 0)]])
-        phase(turns(1, [2, 3]), [[a_qz(1, 0)], [], [tr_qz(1, 2)], [tr_qz(1, 3)]])
-        phase(descriptors(0)[2:], [[], weighs(1, 1, True)])
-        phase(fields(2, 0), [[z_qz(0)], [], [], [a_il(1, 1)]])
-        phase(descriptors(1), [weighs(2, 0) + [a_qz(1, 1)], [a_il(2, 0)], [], [a_qz(2, 0)]])
+        order_scales(0)
+        phase(turns(0, [0]), [[], []])
+        for t in range(SLOTS):
+            order_words(0, t)
+        order_scales(1)
+        phase(fields(0, 0), [[lambda t=t: order_words(1, t)] for t in range(SLOTS)])
+        tr_qz(0, 0)()
+        units = [(0, 0), (0, 1), (1, 0), (1, 1), (2, 0)]
+        passes = [(0, 1), (0, 2), (0, 3), (1, 0)]
+        for n in range(K_PASSES):
+            g, kp = passes[n]
+            phase(turns(g, [kp]), [[], [pj_il(n)]])
+            weigh_on_vector(*units[n], 0)
+            weigh_on_gpsimd(*units[n], range(1, SLOTS))
+            phase(fields(*units[n + 1]), [[], [], [], [pj_qz(n), tr_qz(g, kp)]])
+        z0 = descriptors(0)
+        phase(turns(1, [1]) + z0[:2], [[a_il(0, 0)], [a_il(0, 1)], [tr_qz(1, 1), a_qz(0, 0)], [a_qz(0, 1)]])
+        phase(turns(1, [2]) + z0[2:3], [[a_il(1, 0)], [], [tr_qz(1, 2)]])
+        phase(turns(1, [3]) + z0[3:], [[a_qz(1, 0)], [tr_qz(1, 3)], [a_il(1, 1)]])
+        phase(descriptors(1), [[z_qz(0)] + weighs(2, 0), [a_qz(1, 1), a_il(2, 0)], [], [a_qz(2, 0)]])
         last = weighs(2, 1)
-        phase(fields(2, 1)[:3], [[z_qz(1)], last[:1], last[1:2]])
-        phase(outs(0, range(2)), [[], []])
-        phase(fields(2, 1)[3:], [last[2:]])
-        phase(outs(0, range(2, 4)), [[a_il(2, 1, 0, half), a_il(2, 1, half, BANK)], [a_qz(2, 1, 0, half)]])
-        phase(outs(1, range(4)), [[a_qz(2, 1, half, BANK)], [], [], []])
+        f21 = fields(2, 1)
+        z_qz(1)()
+        phase(f21[:2], [[], last[:1]])
+        phase(outs(0, range(2)) + f21[2:3], [[], [], last[1:2]])
+        phase(outs(0, range(2, 4)) + f21[3:], [[], last[2:3], last[3:]])
+        cuts = [(j * P, (j + 1) * P) for j in range(BANK // P)]
+        il = [a_il(2, 1, *cut) for cut in cuts]
+        qz = [a_qz(2, 1, *cut) for cut in cuts]
+        phase(outs(1, range(4)), [[il[0], il[1], qz[0]], [il[2], qz[1]], [il[3], qz[2]], [qz[3]]])
         for j in range(4):
             out_step(2, j, nc.vector.tensor_copy if j % 2 else nc.scalar.copy)

@@ -18,6 +18,7 @@ ALU = mybir.AluOpType
 
 P = 128
 SLOTS = 4
+RUN = 4
 PASS = P * SLOTS
 BANK = 512
 BANKS = 8
@@ -27,6 +28,9 @@ K_PASSES = K // PASS
 V_CHUNKS = V // BANK
 QUADS = 4
 PROJ_SPLIT = 256
+PROB_BUFS = 8
+AROWS_BUFS = 5
+GB = 3
 
 
 def tile_qubo_replica_flips_s12_kernel(
@@ -50,7 +54,7 @@ def tile_qubo_replica_flips_s12_kernel(
             return keep.tile(shape, dtype, name=name, tag=name, align_bytes=64)
 
         def wide_tile(shape, dtype):
-            return work.tile(shape, dtype, name="wide", tag="wide", bufs=V_CHUNKS, align_bytes=64)
+            return work.tile(shape, dtype, name="wide", tag="wide", bufs=4, align_bytes=64)
 
         def mx_pair(name):
             return kept(name + "_codes", [P, BANK], U32), kept(name + "_scales", [P, BANK], U8)
@@ -72,22 +76,14 @@ def tile_qubo_replica_flips_s12_kernel(
                 in_=rows[:, :, c0:c1].rearrange("p t (c i) -> p c t i", i=4),
             )
 
-        x_raw = [kept("x_raw%d" % g, [P, V_PASSES, 2 * PASS], U8) for g in range(R_PASSES)]
-        xs_raw = kept("xs_raw", [P, V_PASSES, R], U8)
+        x_raw = [kept("x_raw%d" % g, [P, V_PASSES, PASS // 2], I32) for g in range(R_PASSES)]
+        xs_raw = [kept("xs_raw%d" % g, [P, V_PASSES, PASS // 4], I32) for g in range(R_PASSES)]
         j_words = [kept("j_words%d" % c, [P, V_PASSES, 2 * BANK], U8) for c in range(V_CHUNKS)]
         j_scales = [kept("j_scales%d" % n, [P, V_PASSES, w], U8) for n, w in enumerate((BANK, V - BANK))]
-        flip_sb = [
-            [kept("flip%d_%d" % (c, g), [P, SLOTS, BANK], BF16) for g in range(R_PASSES)] for c in range(V_CHUNKS)
-        ]
-        tr_pieces = [(0, 0, 1), (0, 1, 1), (0, 2, 2), (1, 0, 2), (1, 2, 2)]
+        flip_sb = {}
         tr_raw = {}
-        for g, kp, n in tr_pieces:
-            shape = [P, SLOTS, n * PASS]
-            piece = wide_tile(shape, BF16) if n == 2 else kept("tr_first%d" % kp, shape, BF16)
-            for j in range(n):
-                tr_raw[(g, kp + j)] = (piece, j)
         proj_raw = [kept("proj_raw%d" % kp, [P, SLOTS, C], BF16) for kp in range(K_PASSES)]
-        w_raw = kept("w_raw", [P, R_PASSES, SLOTS], BF16)
+        w_raw = kept("w_raw", [P, R_PASSES, RUN * SLOTS], BF16)
         ident = kept("ident", [P, P], F32)
         warm = kept("warm", [P, 1], F32)
 
@@ -100,81 +96,96 @@ def tile_qubo_replica_flips_s12_kernel(
 
         def load_x_words(g):
             src = states_words.bitcast(I32)[:, :, g * PASS // 2 : (g + 1) * PASS // 2]
-            nc.sync.dma_start(out=x_raw[g][:].bitcast(I32), in_=src.rearrange("k p n -> p k n"))
+            nc.sync.dma_start(out=x_raw[g][:], in_=src.rearrange("k p n -> p k n"))
 
         def load_j_words(c):
             src = couplings_words.bitcast(I32)[:, :, c * BANK // 2 : (c + 1) * BANK // 2]
             nc.sync.dma_start(out=j_words[c][:].bitcast(I32), in_=src.rearrange("k p n -> p k n"))
 
-        def load_scale_rows(queue, plane, scales, a, b):
+        def load_scale_rows(plane, scales, a, b, quads=range(QUADS), queue=nc.sync):
             src = scales.bitcast(I32)[:, :, a // 4 : b // 4]
-            for q in range(QUADS):
+            for q in quads:
                 queue.dma_start(
                     out=plane[32 * q : 32 * q + 4, :, :],
                     in_=src[:, 4 * q : 4 * q + 4, :].rearrange("k r n -> r k n"),
                 )
 
-        def load_flip(c, g):
-            src = flip[g * PASS : (g + 1) * PASS, c * BANK : (c + 1) * BANK]
-            nc.sync.dma_start(out=flip_sb[c][g][:], in_=src.rearrange("(p t) v -> p t v", t=SLOTS))
+        def load_flip(g, c0, c1):
+            piece = kept("flip%d_%d" % (g, c0), [P, SLOTS, (c1 - c0) * BANK], BF16)
+            src = flip[g * PASS : (g + 1) * PASS, c0 * BANK : c1 * BANK]
+            src = src.rearrange("(m t i) v -> i m t v", t=SLOTS, i=RUN)
+            for i in range(RUN):
+                nc.sync.dma_start(out=piece[i:P:RUN, :, :], in_=src[i])
+            for c in range(c0, c1):
+                flip_sb[(c, g)] = piece[:, :, (c - c0) * BANK : (c - c0 + 1) * BANK]
 
-        def load_traces(g, kp):
-            piece = tr_raw[(g, kp)][0]
-            src = traces[g * PASS : (g + 1) * PASS, kp * PASS : kp * PASS + piece.shape[2]]
-            nc.sync.dma_start(out=piece[:], in_=src.rearrange("(p t) k -> p t k", t=SLOTS))
+        def load_traces(g, kp, n=2):
+            piece = wide_tile([P, RUN, n * PASS], BF16) if n == 2 else kept("tr_one%d_%d" % (g, kp), [P, RUN, PASS], BF16)
+            src = traces[g * PASS : (g + 1) * PASS, kp * PASS : (kp + n) * PASS]
+            nc.sync.dma_start(out=piece[:], in_=src.rearrange("(a i) k -> a i k", i=RUN))
+            for j in range(n):
+                tr_raw[(g, kp + j)] = (piece, j)
 
         def load_proj(kp):
             src = proj[kp * PASS : (kp + 1) * PASS, :]
             nc.sync.dma_start(out=proj_raw[kp][:], in_=src.rearrange("(p t) c -> p t c", t=SLOTS))
 
-        xs_words = xs_raw[:].bitcast(I32)
-        js_words = [plane[:].bitcast(I32) for plane in j_scales]
-        nc.vector.memset(xs_words, 0)
-        nc.vector.memset(js_words[0], 0)
-        nc.vector.memset(js_words[1], 0)
-        nc.vector.memset(warm[:], 0.0)
-        nc.scalar.activation(out=warm[:], in_=warm[:], func=ACT.Sigmoid)
-        make_identity(nc, ident[:])
+        def load_weight():
+            span = RUN * (SLOTS - 1) + 1
+            src = weight.rearrange("(g m x) -> m g x", g=R_PASSES, x=RUN * SLOTS)
+            for i in range(RUN):
+                nc.gpsimd.dma_start(out=w_raw[i:P:RUN, :, 0:span], in_=src[:, :, i : i + span])
 
-        load_traces(0, 0)
-        load_scale_rows(nc.sync, xs_words, states_scales, 0, R)
+        js_words = [plane[:].bitcast(I32) for plane in j_scales]
+        nc.vector.memset(xs_raw[0][:], 0)
+        nc.vector.memset(js_words[0], 0)
+        nc.vector.memset(warm[:], 0.0)
+        nc.vector.memset(xs_raw[1][:], 0)
+        nc.vector.memset(js_words[1], 0)
+        nc.scalar.activation(out=warm[:], in_=warm[:], func=ACT.Sigmoid)
+
         load_x_words(0)
+        load_scale_rows(xs_raw[0], states_scales, 0, PASS)
         load_j_words(0)
-        load_scale_rows(nc.sync, js_words[0], couplings_scales, 0, BANK)
-        load_scale_rows(nc.gpsimd, js_words[1], couplings_scales, BANK, V)
-        load_flip(0, 0)
+        load_scale_rows(js_words[0], couplings_scales, 0, BANK, range(2))
+        load_scale_rows(js_words[0], couplings_scales, 0, BANK, range(2, 4), nc.gpsimd)
+        make_identity(nc, ident[:])
+        load_weight()
+        load_flip(0, 0, 1)
         load_x_words(1)
-        load_traces(0, 1)
-        nc.sync.dma_start(out=w_raw[:], in_=weight.rearrange("(g p t) -> p g t", g=R_PASSES, t=SLOTS))
+        load_scale_rows(xs_raw[1], states_scales, PASS, R)
         load_proj(0)
-        load_flip(0, 1)
-        load_traces(0, 2)
         load_j_words(1)
+        load_scale_rows(js_words[1], couplings_scales, BANK, V)
+        load_flip(1, 0, 1)
         load_proj(1)
-        load_flip(1, 0)
+        load_traces(0, 0, 1)
+        load_flip(0, 1, 2)
         load_proj(2)
-        load_flip(1, 1)
-        load_traces(1, 0)
+        load_flip(1, 1, 2)
+        load_traces(0, 1, 1)
         load_j_words(2)
         load_proj(3)
-        load_flip(2, 0)
+        load_traces(0, 2)
+        load_flip(0, 2, 3)
+        load_traces(1, 0)
+        load_flip(1, 2, 3)
         load_traces(1, 2)
-        load_flip(2, 1)
 
-        def order_scales(g):
+        def order_states(g):
             nc.vector.tensor_copy(
-                out=x_scales[g][:], in_=xs_raw[:].rearrange("p k (g m t) -> p g k t m", g=R_PASSES, t=SLOTS)[:, g]
+                out=x_scales[g][:].bitcast(I32), in_=xs_raw[g][:].rearrange("p k (m t) -> p k t m", t=SLOTS)
             )
-
-        def order_words(g, t):
             nc.vector.tensor_copy(
-                out=x_codes[g][:, :, t, :].rearrange("p k (m h) -> p k m h", h=2),
-                in_=x_raw[g][:].rearrange("p k (m t h) -> p t k m h", t=SLOTS, h=2)[:, t],
+                out=x_codes[g][:].bitcast(I32).rearrange("p k t (m h) -> p k t m h", h=2),
+                in_=x_raw[g][:].rearrange("p k (m t h) -> p k t m h", t=SLOTS, h=2),
             )
 
         prob = {}
 
-        def field_step(c, g, t):
+        field_banks = {}
+
+        def field_matmuls(c, g, t):
             bank = bank_tile([P, BANK])
             for k in range(V_PASSES):
                 nc.tensor.matmul_mx(
@@ -186,16 +197,22 @@ def tile_qubo_replica_flips_s12_kernel(
                     start=(k == 0),
                     stop=(k == V_PASSES - 1),
                 )
-            pr = work.tile([P, BANK], F32, name="prob", tag="prob", bufs=11)
-            nc.vector.tensor_tensor(out=pr[:], in0=bank[:], in1=flip_sb[c][g][:, t, :], op=ALU.mult)
-            nc.scalar.activation(out=pr[:], in_=pr[:], func=ACT.Sigmoid)
+            field_banks[(c, g, t)] = bank
+
+        def gain(c, g, t):
+            pr = work.tile([P, BANK], F32, name="prob", tag="prob", bufs=PROB_BUFS)
+            nc.vector.tensor_tensor(out=pr[:], in0=field_banks[(c, g, t)][:], in1=flip_sb[(c, g)][:, t, :], op=ALU.mult)
             prob[(c, g, t)] = pr
+
+        def sigmoid(c, g, t):
+            pr = prob[(c, g, t)]
+            nc.scalar.activation(out=pr[:], in_=pr[:], func=ACT.Sigmoid)
 
         tr_grouped = {}
 
-        def turn_step(g, kp, e):
-            if e == 0:
-                tr_grouped[(g, kp)] = grouped_tile("tr_grouped", 3)
+        turn_banks = {}
+
+        def turn_transposes(g, kp, e):
             piece, j = tr_raw[(g, kp)]
             words = piece[:].bitcast(F32)
             w0 = j * (PASS // 2)
@@ -205,10 +222,15 @@ def tile_qubo_replica_flips_s12_kernel(
                     nc.tensor.transpose(
                         bank[:, x, u, :], words[:, 2 * e + x, w0 + u : w0 + PASS // 2 : 2], ident[:]
                     )
+            turn_banks[(g, kp, e)] = bank
+
+        def turn_copy(g, kp, e):
+            if e == 0:
+                tr_grouped[(g, kp)] = grouped_tile("tr_grouped", 4)
             dst = tr_grouped[(g, kp)][:].rearrange("p c t -> p (c t)").bitcast(F32)
             nc.scalar.copy(
-                out=dst.rearrange("p (e x m u) -> p e x m u", e=2, x=2, u=2)[:, e],
-                in_=bank[:].rearrange("p x u m -> p x m u"),
+                out=dst.rearrange("p (t m e w) -> p e m t w", t=SLOTS, e=2, w=4)[:, e],
+                in_=turn_banks[(g, kp, e)][:].rearrange("p x u (m t) -> p m t (x u)", t=SLOTS),
             )
 
         z_grouped = {}
@@ -233,55 +255,63 @@ def tile_qubo_replica_flips_s12_kernel(
             nc.scalar.copy(out=z_grouped[g][:, cols, :], in_=bank[:].rearrange("p t c -> p c t"))
 
         results = {}
+        out_banks = {}
 
-        def out_step(c, j, copy):
+        def out_pass(c, j, g):
             cols = slice(j * P, (j + 1) * P)
-            bank = bank_tile([P, C])
-            for g in range(R_PASSES):
-                nc.tensor.matmul_mx(
-                    out=bank[:],
-                    lhsT=a_q[c][g][0][:, cols].bitcast(FP8X4),
-                    lhsT_scale=a_q[c][g][1][:, cols],
-                    rhs=z_q[g][0][:].bitcast(FP8X4),
-                    rhs_scale=z_q[g][1][:],
-                    start=(g == 0),
-                    stop=(g == R_PASSES - 1),
-                )
+            if g == 0:
+                out_banks[(c, j)] = bank_tile([P, C])
+            nc.tensor.matmul_mx(
+                out=out_banks[(c, j)][:],
+                lhsT=a_q[c][g][0][:, cols].bitcast(FP8X4),
+                lhsT_scale=a_q[c][g][1][:, cols],
+                rhs=z_q[g][0][:].bitcast(FP8X4),
+                rhs_scale=z_q[g][1][:],
+                start=(g == 0),
+                stop=(g == R_PASSES - 1),
+            )
+
+        def out_store(c, j, copy):
             if j == 0:
                 results[c] = wide_tile([P, BANK // P, C], F32)
-            copy(out=results[c][:, j, :], in_=bank[:])
+            copy(out=results[c][:, j, :], in_=out_banks[(c, j)][:])
             nc.sync.dma_start(out=out[c * BANK + j * P : c * BANK + (j + 1) * P, :], in_=results[c][:, j, :])
+
+        def out_step(c, j, copy):
+            for g in range(R_PASSES):
+                out_pass(c, j, g)
+            out_store(c, j, copy)
 
         proj_grouped = {}
 
-        def proj_interleave(kp):
-            proj_grouped[kp] = grouped_tile("grouped", 3)
-            interleave(nc.vector.tensor_copy, proj_grouped[kp], proj_raw[kp], 0, PROJ_SPLIT)
-            interleave(nc.scalar.copy, proj_grouped[kp], proj_raw[kp], PROJ_SPLIT, C)
+        def proj_interleave(kp, copy, c0, c1):
+            if kp not in proj_grouped:
+                proj_grouped[kp] = grouped_tile("grouped", GB)
+            interleave(copy, proj_grouped[kp], proj_raw[kp], c0, c1)
 
         a_rows = {}
         a_grouped = {}
 
         def a_rows_tile(c, g):
-            a_rows[(c, g)] = work.tile([P, SLOTS, BANK], BF16, name="a_rows", tag="a_rows", bufs=4)
+            if (c, g) not in a_rows:
+                a_rows[(c, g)] = work.tile([P, SLOTS, BANK], BF16, name="a_rows", tag="a_rows", bufs=AROWS_BUFS)
+            return a_rows[(c, g)]
 
         def weigh_on_vector(c, g, t):
-            if t == 0:
-                a_rows_tile(c, g)
             nc.vector.tensor_scalar(
-                out=a_rows[(c, g)][:, t, :],
+                out=a_rows_tile(c, g)[:, t, :],
                 in0=prob[(c, g, t)][:],
-                scalar1=w_raw[:, g, t : t + 1],
+                scalar1=w_raw[:, g, RUN * t : RUN * t + 1],
                 scalar2=None,
                 op0=ALU.mult,
             )
 
         def weigh_on_gpsimd(c, g, slots):
             w_col = kept("w_col%d_%d" % (c, g), [P, SLOTS], F32)
-            nc.vector.tensor_copy(out=w_col[:], in_=w_raw[:, g, :])
+            nc.vector.tensor_copy(out=w_col[:], in_=w_raw[:, g, 0 : RUN * (SLOTS - 1) + 1 : RUN])
             for t in slots:
                 nc.gpsimd.tensor_scalar(
-                    out=a_rows[(c, g)][:, t, :],
+                    out=a_rows_tile(c, g)[:, t, :],
                     in0=prob[(c, g, t)][:],
                     scalar1=w_col[:, t : t + 1],
                     scalar2=0.0,
@@ -289,80 +319,148 @@ def tile_qubo_replica_flips_s12_kernel(
                     op1=ALU.add,
                 )
 
-        def a_interleave(c, g, c0, c1):
-            if c0 == 0:
-                a_grouped[(c, g)] = grouped_tile("grouped", 3)
-            interleave(nc.vector.tensor_copy, a_grouped[(c, g)], a_rows[(c, g)], c0, c1)
+        def a_interleave(c, g, c0=0, c1=BANK, copy=nc.vector.tensor_copy):
+            if (c, g) not in a_grouped:
+                a_grouped[(c, g)] = grouped_tile("grouped", GB)
+            interleave(copy, a_grouped[(c, g)], a_rows[(c, g)], c0, c1)
 
-        def fields(c, g):
-            return [lambda t=t: field_step(c, g, t) for t in range(SLOTS)]
+        def a_quantize(c, g, c0=0, c1=BANK):
+            quantize(a_q[c][g], a_grouped[(c, g)], c0, c1)
 
-        def turns(g, kps):
-            return [lambda kp=kp, e=e: turn_step(g, kp, e) for kp in kps for e in range(2)]
-
-        def descriptors(g):
-            return [lambda cq=cq: descriptor_step(g, cq) for cq in range(C // P)]
-
-        def outs(c, js, copy=nc.scalar.copy):
-            return [lambda j=j: out_step(c, j, copy) for j in js]
-
-        def weighs(c, g):
-            return [lambda t=t: weigh_on_vector(c, g, t) for t in range(SLOTS)]
-
-        def a_il(c, g, c0=0, c1=BANK):
-            return lambda: a_interleave(c, g, c0, c1)
-
-        def a_qz(c, g, c0=0, c1=BANK):
-            return lambda: quantize(a_q[c][g], a_grouped[(c, g)], c0, c1)
-
-        def tr_qz(g, kp):
-            return lambda: quantize(tr_q[g][kp], tr_grouped[(g, kp)])
-
-        def pj_il(kp):
-            return lambda: proj_interleave(kp)
-
-        def pj_qz(kp):
-            return lambda: quantize(proj_q[kp], proj_grouped[kp])
-
-        def z_qz(g):
-            return lambda: quantize(z_q[g], z_grouped[g])
-
-        def phase(steps, after):
-            for step, side in zip(steps, after):
-                step()
-                for task in side:
-                    task()
-
-        half = BANK // 2
-        order_scales(0)
-        phase(turns(0, [0]), [[], []])
-        for t in range(SLOTS):
-            order_words(0, t)
-        order_scales(1)
-        phase(fields(0, 0), [[lambda t=t: order_words(1, t)] for t in range(SLOTS)])
-        tr_qz(0, 0)()
-        units = [(0, 0), (0, 1), (1, 0), (1, 1), (2, 0)]
-        passes = [(0, 1), (0, 2), (0, 3), (1, 0)]
-        for n in range(K_PASSES):
+        early = [(0, 0), (1, 0), (2, 0), (0, 1), (1, 1)]
+        passes = [(g, kp) for g in range(R_PASSES) for kp in range(K_PASSES)]
+        def turn(n):
+            for e in range(2):
+                turn_transposes(*passes[n], e)
+                turn_copy(*passes[n], e)
+        def tq(n):
             g, kp = passes[n]
-            phase(turns(g, [kp]), [[], [pj_il(n)]])
-            weigh_on_vector(*units[n], 0)
-            weigh_on_gpsimd(*units[n], range(1, SLOTS))
-            phase(fields(*units[n + 1]), [[], [], [], [pj_qz(n), tr_qz(g, kp)]])
-        z0 = descriptors(0)
-        phase(turns(1, [1]) + z0[:2], [[a_il(0, 0)], [a_il(0, 1)], [tr_qz(1, 1), a_qz(0, 0)], [a_qz(0, 1)]])
-        phase(turns(1, [2]) + z0[2:3], [[a_il(1, 0)], [], [tr_qz(1, 2)]])
-        phase(turns(1, [3]) + z0[3:], [[a_qz(1, 0)], [tr_qz(1, 3)], [a_il(1, 1)]])
-        phase(descriptors(1), [[z_qz(0)] + weighs(2, 0), [a_qz(1, 1), a_il(2, 0)], [], [a_qz(2, 0)]])
-        last = weighs(2, 1)
-        f21 = fields(2, 1)
-        z_qz(1)()
-        phase(f21[:2], [[], last[:1]])
-        phase(outs(0, range(2)) + f21[2:3], [[], [], last[1:2]])
-        phase(outs(0, range(2, 4)) + f21[3:], [[], last[2:3], last[3:]])
+            quantize(tr_q[g][kp], tr_grouped[(g, kp)])
+        def fmm(u, ts=range(SLOTS)):
+            for t in ts:
+                field_matmuls(*u, t)
+        def gs(u, ts=range(SLOTS)):
+            for t in ts:
+                gain(*u, t)
+                sigmoid(*u, t)
+        def wv(u, ts=range(SLOTS)):
+            for t in ts:
+                weigh_on_vector(*u, t)
+        def wg(u, ts=range(SLOTS)):
+            weigh_on_gpsimd(*u, ts)
+        def pil(n):
+            proj_interleave(n, nc.vector.tensor_copy, 0, PROJ_SPLIT)
+            proj_interleave(n, nc.scalar.copy, PROJ_SPLIT, C)
+        def pq(n):
+            quantize(proj_q[n], proj_grouped[n])
+        def zq(g, c0=0, c1=C):
+            quantize(z_q[g], z_grouped[g], c0, c1)
         cuts = [(j * P, (j + 1) * P) for j in range(BANK // P)]
-        il = [a_il(2, 1, *cut) for cut in cuts]
-        qz = [a_qz(2, 1, *cut) for cut in cuts]
-        phase(outs(1, range(4)), [[il[0], il[1], qz[0]], [il[2], qz[1]], [il[3], qz[2]], [qz[3]]])
+
+        units = [(c, g) for c in range(V_CHUNKS) for g in range(R_PASSES)]
+        def tt(n):
+            for e in range(2):
+                turn_transposes(*passes[n], e)
+        def tcp(n):
+            for e in range(2):
+                turn_copy(*passes[n], e)
+        def ail(u, split):
+            a_interleave(*u, 0, split)
+            a_interleave(*u, split, BANK, nc.scalar.copy)
+        def pilv(n):
+            proj_interleave(n, nc.vector.tensor_copy, 0, PROJ_SPLIT)
+        def pils(n):
+            proj_interleave(n, nc.scalar.copy, PROJ_SPLIT, C)
+
+        order_states(0)
+        fmm(units[0])
+        gs(units[0], [0, 1])
+        order_states(1)
+        gs(units[0], [2, 3])
+        for n, u in list(enumerate(units))[1:5]:
+            if n >= 3:
+                tcp(n - 3)
+            pil(n - 1)
+            if n >= 4:
+                tq(n - 4)
+            if n >= 2:
+                pq(n - 2)
+            fmm(u)
+            if n >= 2:
+                tt(n - 2)
+            wg(units[n - 1], range(3))
+            if n < 4:
+                gs(u)
+            else:
+                for t in range(SLOTS):
+                    gain(*u, t)
+            wv(units[n - 1], [3])
+        last = units[5]
+        tt(3)
+        tcp(2)
+        tq(1)
+        pq(3)
+        tcp(3)
+        for t in range(SLOTS):
+            sigmoid(*units[4], t)
+        fmm(last, [0, 1])
+        tq(2)
+        tt(4)
+        tq(3)
+        tcp(4)
+        a_interleave(*units[0])
+        descriptor_step(0, 0)
+        wg(units[4], range(2))
+        gs(last, [0, 1])
+        wv(units[4], [2, 3])
+        tt(5)
+        tcp(5)
+        a_quantize(*units[0])
+        tq(4)
+        descriptor_step(0, 1)
+        a_interleave(*units[1])
+        tt(6)
+        tcp(6)
+        tq(5)
+        descriptor_step(0, 2)
+        tq(6)
+        a_quantize(*units[1])
+        tt(7)
+        tcp(7)
+        wv(last, [0, 1])
+        descriptor_step(0, 3)
+        tq(7)
+        a_interleave(*units[2])
+        ail(units[3], 256)
+        descriptor_step(1, 0)
+        zq(0)
+        a_quantize(*units[2])
+        ail(units[4], 256)
+        descriptor_step(1, 1)
+        a_quantize(*units[3])
+        zq(1, *cuts[0])
+        descriptor_step(1, 2)
+        a_quantize(*units[4])
+        zq(1, *cuts[1])
+        descriptor_step(1, 3)
+        zq(1, *cuts[2])
+        fmm(last, [2])
+        zq(1, *cuts[3])
+        gs(last, [2])
+        for j in range(2):
+            out_step(0, j, nc.scalar.copy if j else nc.vector.tensor_copy)
+        fmm(last, [3])
+        wv(last, [2])
+        gs(last, [3])
+        for j in range(2, 4):
+            out_step(0, j, nc.vector.tensor_copy if j == 2 else nc.scalar.copy)
+        wv(last, [3])
+        a_interleave(*last, *cuts[0])
         for j in range(4):
-            out_step(2, j, nc.vector.tensor_copy if j % 2 else nc.scalar.copy)
+            if j < 3:
+                a_interleave(*last, *cuts[j + 1])
+            a_quantize(*last, *cuts[j])
+        for j in range(4):
+            out_step(1, j, nc.scalar.copy)
+        for j in range(4):
+            out_step(2, j, nc.vector.tensor_copy if j % 2 == 0 else nc.scalar.copy)

@@ -21,16 +21,23 @@ SLOTS = 4
 RUN = 4
 PASS = P * SLOTS
 BANK = 512
+HALF = BANK // 2
 BANKS = 8
+QUADS = 4
 R_PASSES = R // PASS
 V_PASSES = V // PASS
 K_PASSES = K // PASS
 V_CHUNKS = V // BANK
-QUADS = 4
-PROJ_SPLIT = 256
+TILES = BANK // P
+
+SHARE = 256
+GPSIMD_SLOTS = 3
+
+WIDE_BUFS = 3
 PROB_BUFS = 8
-AROWS_BUFS = 5
-GB = 3
+A_ROWS_BUFS = 5
+GROUPED_BUFS = 4
+TURNED_BUFS = 4
 
 
 def tile_qubo_replica_flips_s12_kernel(
@@ -39,7 +46,7 @@ def tile_qubo_replica_flips_s12_kernel(
     nc = tc.nc
     with ExitStack() as ctx:
         keep = ctx.enter_context(tc.tile_pool(name="keep", bufs=1))
-        work = ctx.enter_context(tc.tile_pool(name="work", bufs=4))
+        work = ctx.enter_context(tc.tile_pool(name="work", bufs=1))
         psum = ctx.enter_context(tc.psum_pool(name="psum", bufs=1))
         ctx.enter_context(tc.manual_schedule())
 
@@ -53,14 +60,14 @@ def tile_qubo_replica_flips_s12_kernel(
         def kept(name, shape, dtype):
             return keep.tile(shape, dtype, name=name, tag=name, align_bytes=64)
 
-        def wide_tile(shape, dtype):
-            return work.tile(shape, dtype, name="wide", tag="wide", bufs=4, align_bytes=64)
+        def pooled(tag, bufs, shape, dtype):
+            return work.tile(shape, dtype, name=tag, tag=tag, bufs=bufs, align_bytes=64)
 
         def mx_pair(name):
             return kept(name + "_codes", [P, BANK], U32), kept(name + "_scales", [P, BANK], U8)
 
         def grouped_tile(tag, bufs):
-            return work.tile([P, BANK, SLOTS], BF16, name=tag, tag=tag, bufs=bufs, align_bytes=64)
+            return pooled(tag, bufs, [P, BANK, SLOTS], BF16)
 
         def quantize(pair, grouped, c0=0, c1=BANK):
             codes, scales = pair
@@ -70,29 +77,27 @@ def tile_qubo_replica_flips_s12_kernel(
                 in_=grouped[:, c0:c1, :].rearrange("p c t -> p (c t)"),
             )
 
-        def interleave(copy, grouped, rows, c0=0, c1=BANK):
+        def interleave(copy, grouped, rows, c0, c1):
             copy(
                 out=grouped[:, c0:c1, :].rearrange("p (c i) t -> p c t i", i=4),
                 in_=rows[:, :, c0:c1].rearrange("p t (c i) -> p c t i", i=4),
             )
 
+        units = [(c, g) for c in range(V_CHUNKS) for g in range(R_PASSES)]
+        trace_passes = [(g, kp) for g in range(R_PASSES) for kp in range(K_PASSES)]
+        column_tiles = [(j * P, (j + 1) * P) for j in range(TILES)]
+
         x_raw = [kept("x_raw%d" % g, [P, V_PASSES, PASS // 2], I32) for g in range(R_PASSES)]
         xs_raw = [kept("xs_raw%d" % g, [P, V_PASSES, PASS // 4], I32) for g in range(R_PASSES)]
         j_words = [kept("j_words%d" % c, [P, V_PASSES, 2 * BANK], U8) for c in range(V_CHUNKS)]
-        j_scales = [kept("j_scales%d" % n, [P, V_PASSES, w], U8) for n, w in enumerate((BANK, V - BANK))]
-        flip_sb = {}
-        tr_raw = {}
+        js_first = kept("js_first", [P, V_PASSES, BANK], U8)
+        js_rest = kept("js_rest", [P, V_PASSES, V - BANK], U8)
         proj_raw = [kept("proj_raw%d" % kp, [P, SLOTS, C], BF16) for kp in range(K_PASSES)]
         w_raw = kept("w_raw", [P, R_PASSES, RUN * SLOTS], BF16)
         ident = kept("ident", [P, P], F32)
         warm = kept("warm", [P, 1], F32)
-
-        x_codes = [kept("x_codes%d" % g, [P, V_PASSES, SLOTS, 2 * P], U8) for g in range(R_PASSES)]
-        x_scales = [kept("x_scales%d" % g, [P, V_PASSES, SLOTS, P], U8) for g in range(R_PASSES)]
-        proj_q = [mx_pair("proj_q%d" % kp) for kp in range(K_PASSES)]
-        tr_q = [[mx_pair("tr_q%d_%d" % (g, kp)) for kp in range(K_PASSES)] for g in range(R_PASSES)]
-        z_q = [mx_pair("z_q%d" % g) for g in range(R_PASSES)]
-        a_q = [[mx_pair("a_q%d_%d" % (c, g)) for g in range(R_PASSES)] for c in range(V_CHUNKS)]
+        flip_sb = {}
+        traces_raw = {}
 
         def load_x_words(g):
             src = states_words.bitcast(I32)[:, :, g * PASS // 2 : (g + 1) * PASS // 2]
@@ -102,151 +107,237 @@ def tile_qubo_replica_flips_s12_kernel(
             src = couplings_words.bitcast(I32)[:, :, c * BANK // 2 : (c + 1) * BANK // 2]
             nc.sync.dma_start(out=j_words[c][:].bitcast(I32), in_=src.rearrange("k p n -> p k n"))
 
-        def load_scale_rows(plane, scales, a, b, quads=range(QUADS), queue=nc.sync):
-            src = scales.bitcast(I32)[:, :, a // 4 : b // 4]
+        def load_scale_rows(queue, plane, scales, n0, n1, quads):
+            src = scales.bitcast(I32)[:, :, n0 // 4 : n1 // 4]
             for q in quads:
                 queue.dma_start(
                     out=plane[32 * q : 32 * q + 4, :, :],
                     in_=src[:, 4 * q : 4 * q + 4, :].rearrange("k r n -> r k n"),
                 )
 
-        def load_flip(g, c0, c1):
-            piece = kept("flip%d_%d" % (g, c0), [P, SLOTS, (c1 - c0) * BANK], BF16)
-            src = flip[g * PASS : (g + 1) * PASS, c0 * BANK : c1 * BANK]
+        def load_flip(c, g):
+            flip_sb[(c, g)] = kept("flip%d_%d" % (c, g), [P, SLOTS, BANK], BF16)
+            src = flip[g * PASS : (g + 1) * PASS, c * BANK : (c + 1) * BANK]
             src = src.rearrange("(m t i) v -> i m t v", t=SLOTS, i=RUN)
             for i in range(RUN):
-                nc.sync.dma_start(out=piece[i:P:RUN, :, :], in_=src[i])
-            for c in range(c0, c1):
-                flip_sb[(c, g)] = piece[:, :, (c - c0) * BANK : (c - c0 + 1) * BANK]
+                nc.sync.dma_start(out=flip_sb[(c, g)][i:P:RUN, :, :], in_=src[i])
 
-        def load_traces(g, kp, n=2):
-            piece = wide_tile([P, RUN, n * PASS], BF16) if n == 2 else kept("tr_one%d_%d" % (g, kp), [P, RUN, PASS], BF16)
-            src = traces[g * PASS : (g + 1) * PASS, kp * PASS : (kp + n) * PASS]
+        def load_traces(piece, g, kp):
+            width = piece.shape[2]
+            src = traces[g * PASS : (g + 1) * PASS, kp * PASS : kp * PASS + width]
             nc.sync.dma_start(out=piece[:], in_=src.rearrange("(a i) k -> a i k", i=RUN))
-            for j in range(n):
-                tr_raw[(g, kp + j)] = (piece, j)
+            for j in range(width // PASS):
+                traces_raw[(g, kp + j)] = (piece, j)
+
+        def load_traces_pass(g, kp):
+            load_traces(kept("traces%d_%d" % (g, kp), [P, RUN, PASS], BF16), g, kp)
+
+        def load_traces_pair(g, kp):
+            load_traces(pooled("wide", WIDE_BUFS, [P, RUN, 2 * PASS], BF16), g, kp)
 
         def load_proj(kp):
             src = proj[kp * PASS : (kp + 1) * PASS, :]
             nc.sync.dma_start(out=proj_raw[kp][:], in_=src.rearrange("(p t) c -> p t c", t=SLOTS))
 
+        weight_span = RUN * (SLOTS - 1) + 1
+
         def load_weight():
-            span = RUN * (SLOTS - 1) + 1
             src = weight.rearrange("(g m x) -> m g x", g=R_PASSES, x=RUN * SLOTS)
             for i in range(RUN):
-                nc.gpsimd.dma_start(out=w_raw[i:P:RUN, :, 0:span], in_=src[:, :, i : i + span])
+                nc.gpsimd.dma_start(out=w_raw[i:P:RUN, :, 0:weight_span], in_=src[:, :, i : i + weight_span])
 
-        js_words = [plane[:].bitcast(I32) for plane in j_scales]
+        js_first_words = js_first[:].bitcast(I32)
+        js_rest_words = js_rest[:].bitcast(I32)
+        nc.vector.memset(js_first_words, 0)
         nc.vector.memset(xs_raw[0][:], 0)
-        nc.vector.memset(js_words[0], 0)
         nc.vector.memset(warm[:], 0.0)
         nc.vector.memset(xs_raw[1][:], 0)
-        nc.vector.memset(js_words[1], 0)
+        nc.vector.memset(js_rest_words, 0)
         nc.scalar.activation(out=warm[:], in_=warm[:], func=ACT.Sigmoid)
 
         load_x_words(0)
-        load_scale_rows(xs_raw[0], states_scales, 0, PASS)
+        load_scale_rows(nc.sync, xs_raw[0], states_scales, 0, PASS, range(QUADS))
         load_j_words(0)
-        load_scale_rows(js_words[0], couplings_scales, 0, BANK, range(2))
-        load_scale_rows(js_words[0], couplings_scales, 0, BANK, range(2, 4), nc.gpsimd)
+        load_scale_rows(nc.sync, js_first_words, couplings_scales, 0, BANK, range(QUADS // 2))
+        load_scale_rows(nc.gpsimd, js_first_words, couplings_scales, 0, BANK, range(QUADS // 2, QUADS))
         make_identity(nc, ident[:])
         load_weight()
-        load_flip(0, 0, 1)
+        load_flip(*units[0])
         load_x_words(1)
-        load_scale_rows(xs_raw[1], states_scales, PASS, R)
+        load_scale_rows(nc.sync, xs_raw[1], states_scales, PASS, R, range(QUADS))
         load_proj(0)
+        load_flip(*units[1])
         load_j_words(1)
-        load_scale_rows(js_words[1], couplings_scales, BANK, V)
-        load_flip(1, 0, 1)
+        load_scale_rows(nc.sync, js_rest_words, couplings_scales, BANK, V, range(QUADS))
         load_proj(1)
-        load_traces(0, 0, 1)
-        load_flip(0, 1, 2)
+        load_traces_pass(0, 0)
+        load_flip(*units[2])
         load_proj(2)
-        load_flip(1, 1, 2)
-        load_traces(0, 1, 1)
+        load_flip(*units[3])
+        load_traces_pass(0, 1)
         load_j_words(2)
         load_proj(3)
-        load_traces(0, 2)
-        load_flip(0, 2, 3)
-        load_traces(1, 0)
-        load_flip(1, 2, 3)
-        load_traces(1, 2)
+        load_traces_pair(0, 2)
+        load_flip(*units[4])
+        load_traces_pair(1, 0)
+        load_flip(*units[5])
+        load_traces_pair(1, 2)
+
+        x_codes = [kept("x_codes%d" % g, [P, SLOTS, V_PASSES, 2 * P], U8) for g in range(R_PASSES)]
+        x_scales = [kept("x_scales%d" % g, [P, SLOTS, V_PASSES, P], U8) for g in range(R_PASSES)]
+        proj_q = [mx_pair("proj_q%d" % kp) for kp in range(K_PASSES)]
+        traces_q = {(g, kp): mx_pair("traces_q%d_%d" % (g, kp)) for g, kp in trace_passes}
+        z_q = [mx_pair("z_q%d" % g) for g in range(R_PASSES)]
+        a_q = {(c, g): mx_pair("a_q%d_%d" % (c, g)) for c, g in units}
 
         def order_states(g):
             nc.vector.tensor_copy(
-                out=x_scales[g][:].bitcast(I32), in_=xs_raw[g][:].rearrange("p k (m t) -> p k t m", t=SLOTS)
+                out=x_codes[g][:].bitcast(I32).rearrange("p t k (m h) -> p t (k m) h", h=2),
+                in_=x_raw[g][:].rearrange("p k (m t h) -> p t (k m) h", t=SLOTS, h=2),
             )
             nc.vector.tensor_copy(
-                out=x_codes[g][:].bitcast(I32).rearrange("p k t (m h) -> p k t m h", h=2),
-                in_=x_raw[g][:].rearrange("p k (m t h) -> p k t m h", t=SLOTS, h=2),
+                out=x_scales[g][:].bitcast(I32).rearrange("p t k m -> p t (k m)"),
+                in_=xs_raw[g][:].rearrange("p k (m t) -> p t (k m)", t=SLOTS),
             )
 
-        prob = {}
+        def slot_steps(unit):
+            return [(unit, t, 1, 0, BANK) for t in range(SLOTS)]
+
+        def half_steps(unit, h):
+            return [(unit, t, 2, h * HALF, HALF) for t in range(0, SLOTS, 2)]
 
         field_banks = {}
+        prob = {}
+        a_rows = {}
+        a_grouped = {}
 
-        def field_matmuls(c, g, t):
-            bank = bank_tile([P, BANK])
-            for k in range(V_PASSES):
-                nc.tensor.matmul_mx(
-                    out=bank[:],
-                    lhsT=x_codes[g][:, k, t, :].bitcast(FP4X4),
-                    lhsT_scale=x_scales[g][:, k, t, :],
-                    rhs=j_words[c][:, k, :].bitcast(FP4X4),
-                    rhs_scale=j_scales[0][:, k, :] if c == 0 else j_scales[1][:, k, (c - 1) * BANK : c * BANK],
-                    start=(k == 0),
-                    stop=(k == V_PASSES - 1),
+        def field(steps):
+            for step in steps:
+                (c, g), t0, slots, v0, width = step
+                j_scales, s0 = (js_first, v0) if c == 0 else (js_rest, (c - 1) * BANK + v0)
+                field_banks[step] = bank_tile([P, slots, width])
+                for e in range(slots):
+                    for k in range(V_PASSES):
+                        nc.tensor.matmul_mx(
+                            out=field_banks[step][:, e, :],
+                            lhsT=x_codes[g][:, t0 + e, k, :].bitcast(FP4X4),
+                            lhsT_scale=x_scales[g][:, t0 + e, k, :],
+                            rhs=j_words[c][:, k, 2 * v0 : 2 * (v0 + width)].bitcast(FP4X4),
+                            rhs_scale=j_scales[:, k, s0 : s0 + width],
+                            start=(k == 0),
+                            stop=(k == V_PASSES - 1),
+                        )
+
+        def gain(steps):
+            for step in steps:
+                unit, t0, slots, v0, width = step
+                prob[step] = pooled("prob", PROB_BUFS, [P, slots, width], F32)
+                nc.vector.tensor_tensor(
+                    out=prob[step][:],
+                    in0=field_banks[step][:],
+                    in1=flip_sb[unit][:, t0 : t0 + slots, v0 : v0 + width],
+                    op=ALU.mult,
                 )
-            field_banks[(c, g, t)] = bank
 
-        def gain(c, g, t):
-            pr = work.tile([P, BANK], F32, name="prob", tag="prob", bufs=PROB_BUFS)
-            nc.vector.tensor_tensor(out=pr[:], in0=field_banks[(c, g, t)][:], in1=flip_sb[(c, g)][:, t, :], op=ALU.mult)
-            prob[(c, g, t)] = pr
+        def sigmoid(steps):
+            for step in steps:
+                nc.scalar.activation(out=prob[step][:], in_=prob[step][:], func=ACT.Sigmoid)
 
-        def sigmoid(c, g, t):
-            pr = prob[(c, g, t)]
-            nc.scalar.activation(out=pr[:], in_=pr[:], func=ACT.Sigmoid)
+        def gain_and_sigmoid(steps):
+            for step in steps:
+                gain([step])
+                sigmoid([step])
 
-        tr_grouped = {}
+        def a_rows_tile(unit):
+            if unit not in a_rows:
+                a_rows[unit] = pooled("a_rows", A_ROWS_BUFS, [P, SLOTS, BANK], BF16)
+            return a_rows[unit]
+
+        def weigh_on_vector(steps):
+            for step in steps:
+                unit, t0, slots, v0, width = step
+                for e in range(slots):
+                    t = t0 + e
+                    nc.vector.tensor_scalar(
+                        out=a_rows_tile(unit)[:, t, v0 : v0 + width],
+                        in0=prob[step][:, e, :],
+                        scalar1=w_raw[:, unit[1], RUN * t : RUN * t + 1],
+                        scalar2=None,
+                        op0=ALU.mult,
+                    )
+
+        def weigh_on_gpsimd(steps):
+            unit = steps[0][0]
+            w_col = kept("w_col%d_%d" % unit, [P, SLOTS], F32)
+            nc.vector.tensor_copy(out=w_col[:], in_=w_raw[:, unit[1], 0:weight_span:RUN])
+            for step in steps:
+                t = step[1]
+                nc.gpsimd.tensor_scalar(
+                    out=a_rows_tile(unit)[:, t, :],
+                    in0=prob[step][:, 0, :],
+                    scalar1=w_col[:, t : t + 1],
+                    scalar2=0.0,
+                    op0=ALU.mult,
+                    op1=ALU.add,
+                )
+
+        def a_interleave(unit, c0=0, c1=BANK, copy=nc.vector.tensor_copy):
+            if unit not in a_grouped:
+                a_grouped[unit] = grouped_tile("grouped", GROUPED_BUFS)
+            interleave(copy, a_grouped[unit], a_rows[unit], c0, c1)
+
+        def a_quantize(unit, c0=0, c1=BANK):
+            quantize(a_q[unit], a_grouped[unit], c0, c1)
 
         turn_banks = {}
-
-        def turn_transposes(g, kp, e):
-            piece, j = tr_raw[(g, kp)]
-            words = piece[:].bitcast(F32)
-            w0 = j * (PASS // 2)
-            bank = bank_tile([P, 2, 2, P])
-            for x in range(2):
-                for u in range(2):
-                    nc.tensor.transpose(
-                        bank[:, x, u, :], words[:, 2 * e + x, w0 + u : w0 + PASS // 2 : 2], ident[:]
-                    )
-            turn_banks[(g, kp, e)] = bank
-
-        def turn_copy(g, kp, e):
-            if e == 0:
-                tr_grouped[(g, kp)] = grouped_tile("tr_grouped", 4)
-            dst = tr_grouped[(g, kp)][:].rearrange("p c t -> p (c t)").bitcast(F32)
-            nc.scalar.copy(
-                out=dst.rearrange("p (t m e w) -> p e m t w", t=SLOTS, e=2, w=4)[:, e],
-                in_=turn_banks[(g, kp, e)][:].rearrange("p x u (m t) -> p m t (x u)", t=SLOTS),
-            )
-
+        turned = {}
+        proj_grouped = {}
         z_grouped = {}
 
-        def descriptor_step(g, cq):
-            if cq == 0:
-                z_grouped[g] = grouped_tile("z_grouped", 2)
-            cols = slice(cq * P, (cq + 1) * P)
+        def turn(n):
+            piece, j = traces_raw[trace_passes[n]]
+            words = piece[:].bitcast(F32)
+            w0 = j * (PASS // 2)
+            for e in range(2):
+                turn_banks[(n, e)] = bank_tile([P, 2, 2, P])
+                for x in range(2):
+                    for u in range(2):
+                        nc.tensor.transpose(
+                            turn_banks[(n, e)][:, x, u, :], words[:, 2 * e + x, w0 + u : w0 + PASS // 2 : 2], ident[:]
+                        )
+
+        def turn_copy(n):
+            turned[n] = grouped_tile("turned", TURNED_BUFS)
+            dst = turned[n][:].rearrange("p c t -> p (c t)").bitcast(F32)
+            for e in range(2):
+                nc.scalar.copy(
+                    out=dst.rearrange("p (t m e w) -> p e m t w", t=SLOTS, e=2, w=4)[:, e],
+                    in_=turn_banks[(n, e)][:].rearrange("p x u (m t) -> p m t (x u)", t=SLOTS),
+                )
+
+        def traces_quantize(n):
+            quantize(traces_q[trace_passes[n]], turned[n])
+
+        def proj_interleave(kp):
+            proj_grouped[kp] = grouped_tile("grouped", GROUPED_BUFS)
+            interleave(nc.vector.tensor_copy, proj_grouped[kp], proj_raw[kp], 0, SHARE)
+            interleave(nc.scalar.copy, proj_grouped[kp], proj_raw[kp], SHARE, C)
+
+        def proj_quantize(kp):
+            quantize(proj_q[kp], proj_grouped[kp])
+
+        def descriptors(g, j):
+            if j == 0:
+                z_grouped[g] = grouped_tile("z_grouped", R_PASSES)
+            cols = slice(*column_tiles[j])
             bank = bank_tile([P, SLOTS, P])
             for t in range(SLOTS):
-                reps = slice(t * P, (t + 1) * P)
+                replicas = slice(t * P, (t + 1) * P)
                 for kp in range(K_PASSES):
                     nc.tensor.matmul_mx(
                         out=bank[:, t, :],
-                        lhsT=tr_q[g][kp][0][:, reps].bitcast(FP8X4),
-                        lhsT_scale=tr_q[g][kp][1][:, reps],
+                        lhsT=traces_q[(g, kp)][0][:, replicas].bitcast(FP8X4),
+                        lhsT_scale=traces_q[(g, kp)][1][:, replicas],
                         rhs=proj_q[kp][0][:, cols].bitcast(FP8X4),
                         rhs_scale=proj_q[kp][1][:, cols],
                         start=(kp == 0),
@@ -254,17 +345,20 @@ def tile_qubo_replica_flips_s12_kernel(
                     )
             nc.scalar.copy(out=z_grouped[g][:, cols, :], in_=bank[:].rearrange("p t c -> p c t"))
 
-        results = {}
+        def z_quantize(g, c0=0, c1=C):
+            quantize(z_q[g], z_grouped[g], c0, c1)
+
         out_banks = {}
+        results = {}
 
         def out_pass(c, j, g):
-            cols = slice(j * P, (j + 1) * P)
+            cols = slice(*column_tiles[j])
             if g == 0:
                 out_banks[(c, j)] = bank_tile([P, C])
             nc.tensor.matmul_mx(
                 out=out_banks[(c, j)][:],
-                lhsT=a_q[c][g][0][:, cols].bitcast(FP8X4),
-                lhsT_scale=a_q[c][g][1][:, cols],
+                lhsT=a_q[(c, g)][0][:, cols].bitcast(FP8X4),
+                lhsT_scale=a_q[(c, g)][1][:, cols],
                 rhs=z_q[g][0][:].bitcast(FP8X4),
                 rhs_scale=z_q[g][1][:],
                 start=(g == 0),
@@ -273,194 +367,120 @@ def tile_qubo_replica_flips_s12_kernel(
 
         def out_store(c, j, copy):
             if j == 0:
-                results[c] = wide_tile([P, BANK // P, C], F32)
+                results[c] = pooled("wide", WIDE_BUFS, [P, TILES, C], F32)
             copy(out=results[c][:, j, :], in_=out_banks[(c, j)][:])
             nc.sync.dma_start(out=out[c * BANK + j * P : c * BANK + (j + 1) * P, :], in_=results[c][:, j, :])
 
-        def out_step(c, j, copy):
+        def out_tile(c, j, copy):
             for g in range(R_PASSES):
                 out_pass(c, j, g)
             out_store(c, j, copy)
 
-        proj_grouped = {}
-
-        def proj_interleave(kp, copy, c0, c1):
-            if kp not in proj_grouped:
-                proj_grouped[kp] = grouped_tile("grouped", GB)
-            interleave(copy, proj_grouped[kp], proj_raw[kp], c0, c1)
-
-        a_rows = {}
-        a_grouped = {}
-
-        def a_rows_tile(c, g):
-            if (c, g) not in a_rows:
-                a_rows[(c, g)] = work.tile([P, SLOTS, BANK], BF16, name="a_rows", tag="a_rows", bufs=AROWS_BUFS)
-            return a_rows[(c, g)]
-
-        def weigh_on_vector(c, g, t):
-            nc.vector.tensor_scalar(
-                out=a_rows_tile(c, g)[:, t, :],
-                in0=prob[(c, g, t)][:],
-                scalar1=w_raw[:, g, RUN * t : RUN * t + 1],
-                scalar2=None,
-                op0=ALU.mult,
-            )
-
-        def weigh_on_gpsimd(c, g, slots):
-            w_col = kept("w_col%d_%d" % (c, g), [P, SLOTS], F32)
-            nc.vector.tensor_copy(out=w_col[:], in_=w_raw[:, g, 0 : RUN * (SLOTS - 1) + 1 : RUN])
-            for t in slots:
-                nc.gpsimd.tensor_scalar(
-                    out=a_rows_tile(c, g)[:, t, :],
-                    in0=prob[(c, g, t)][:],
-                    scalar1=w_col[:, t : t + 1],
-                    scalar2=0.0,
-                    op0=ALU.mult,
-                    op1=ALU.add,
-                )
-
-        def a_interleave(c, g, c0=0, c1=BANK, copy=nc.vector.tensor_copy):
-            if (c, g) not in a_grouped:
-                a_grouped[(c, g)] = grouped_tile("grouped", GB)
-            interleave(copy, a_grouped[(c, g)], a_rows[(c, g)], c0, c1)
-
-        def a_quantize(c, g, c0=0, c1=BANK):
-            quantize(a_q[c][g], a_grouped[(c, g)], c0, c1)
-
-        early = [(0, 0), (1, 0), (2, 0), (0, 1), (1, 1)]
-        passes = [(g, kp) for g in range(R_PASSES) for kp in range(K_PASSES)]
-        def turn(n):
-            for e in range(2):
-                turn_transposes(*passes[n], e)
-                turn_copy(*passes[n], e)
-        def tq(n):
-            g, kp = passes[n]
-            quantize(tr_q[g][kp], tr_grouped[(g, kp)])
-        def fmm(u, ts=range(SLOTS)):
-            for t in ts:
-                field_matmuls(*u, t)
-        def gs(u, ts=range(SLOTS)):
-            for t in ts:
-                gain(*u, t)
-                sigmoid(*u, t)
-        def wv(u, ts=range(SLOTS)):
-            for t in ts:
-                weigh_on_vector(*u, t)
-        def wg(u, ts=range(SLOTS)):
-            weigh_on_gpsimd(*u, ts)
-        def pil(n):
-            proj_interleave(n, nc.vector.tensor_copy, 0, PROJ_SPLIT)
-            proj_interleave(n, nc.scalar.copy, PROJ_SPLIT, C)
-        def pq(n):
-            quantize(proj_q[n], proj_grouped[n])
-        def zq(g, c0=0, c1=C):
-            quantize(z_q[g], z_grouped[g], c0, c1)
-        cuts = [(j * P, (j + 1) * P) for j in range(BANK // P)]
-
-        units = [(c, g) for c in range(V_CHUNKS) for g in range(R_PASSES)]
-        def tt(n):
-            for e in range(2):
-                turn_transposes(*passes[n], e)
-        def tcp(n):
-            for e in range(2):
-                turn_copy(*passes[n], e)
-        def ail(u, split):
-            a_interleave(*u, 0, split)
-            a_interleave(*u, split, BANK, nc.scalar.copy)
-        def pilv(n):
-            proj_interleave(n, nc.vector.tensor_copy, 0, PROJ_SPLIT)
-        def pils(n):
-            proj_interleave(n, nc.scalar.copy, PROJ_SPLIT, C)
+        on_vector, on_scalar = nc.vector.tensor_copy, nc.scalar.copy
+        last = units[-1]
+        before_last = units[-2]
 
         order_states(0)
-        fmm(units[0])
-        gs(units[0], [0, 1])
+        field(slot_steps(units[0]))
+        gain_and_sigmoid(slot_steps(units[0])[:2])
         order_states(1)
-        gs(units[0], [2, 3])
-        for n, u in list(enumerate(units))[1:5]:
+        gain_and_sigmoid(slot_steps(units[0])[2:])
+
+        for n in range(1, len(units) - 1):
+            unit, previous = units[n], units[n - 1]
+            closing = unit == before_last
             if n >= 3:
-                tcp(n - 3)
-            pil(n - 1)
-            if n >= 4:
-                tq(n - 4)
+                turn_copy(n - 3)
+            proj_interleave(n - 1)
+            if closing:
+                traces_quantize(0)
             if n >= 2:
-                pq(n - 2)
-            fmm(u)
+                proj_quantize(n - 2)
+            if closing:
+                traces_quantize(1)
+            if n == 2:
+                a_interleave(units[0])
+            if n == 3:
+                a_quantize(units[0])
+            field(slot_steps(unit))
             if n >= 2:
-                tt(n - 2)
-            wg(units[n - 1], range(3))
-            if n < 4:
-                gs(u)
+                turn(n - 2)
+            weigh_on_gpsimd(slot_steps(previous)[:GPSIMD_SLOTS])
+            if closing:
+                gain(slot_steps(unit))
             else:
-                for t in range(SLOTS):
-                    gain(*u, t)
-            wv(units[n - 1], [3])
-        last = units[5]
-        tt(3)
-        tcp(2)
-        tq(1)
-        pq(3)
-        tcp(3)
-        for t in range(SLOTS):
-            sigmoid(*units[4], t)
-        fmm(last, [0, 1])
-        tq(2)
-        tt(4)
-        tq(3)
-        tcp(4)
-        a_interleave(*units[0])
-        descriptor_step(0, 0)
-        wg(units[4], range(2))
-        gs(last, [0, 1])
-        wv(units[4], [2, 3])
-        tt(5)
-        tcp(5)
-        a_quantize(*units[0])
-        tq(4)
-        descriptor_step(0, 1)
-        a_interleave(*units[1])
-        tt(6)
-        tcp(6)
-        tq(5)
-        descriptor_step(0, 2)
-        tq(6)
-        a_quantize(*units[1])
-        tt(7)
-        tcp(7)
-        wv(last, [0, 1])
-        descriptor_step(0, 3)
-        tq(7)
-        a_interleave(*units[2])
-        ail(units[3], 256)
-        descriptor_step(1, 0)
-        zq(0)
-        a_quantize(*units[2])
-        ail(units[4], 256)
-        descriptor_step(1, 1)
-        a_quantize(*units[3])
-        zq(1, *cuts[0])
-        descriptor_step(1, 2)
-        a_quantize(*units[4])
-        zq(1, *cuts[1])
-        descriptor_step(1, 3)
-        zq(1, *cuts[2])
-        fmm(last, [2])
-        zq(1, *cuts[3])
-        gs(last, [2])
-        for j in range(2):
-            out_step(0, j, nc.scalar.copy if j else nc.vector.tensor_copy)
-        fmm(last, [3])
-        wv(last, [2])
-        gs(last, [3])
-        for j in range(2, 4):
-            out_step(0, j, nc.vector.tensor_copy if j == 2 else nc.scalar.copy)
-        wv(last, [3])
-        a_interleave(*last, *cuts[0])
-        for j in range(4):
-            if j < 3:
-                a_interleave(*last, *cuts[j + 1])
-            a_quantize(*last, *cuts[j])
-        for j in range(4):
-            out_step(1, j, nc.scalar.copy)
-        for j in range(4):
-            out_step(2, j, nc.vector.tensor_copy if j % 2 == 0 else nc.scalar.copy)
+                gain_and_sigmoid(slot_steps(unit))
+            weigh_on_vector(slot_steps(previous)[GPSIMD_SLOTS:])
+
+        turn(3)
+        turn_copy(2)
+        proj_quantize(K_PASSES - 1)
+        turn_copy(3)
+        sigmoid(slot_steps(before_last))
+        field(half_steps(last, 0))
+        traces_quantize(2)
+        turn(4)
+        turn(5)
+        traces_quantize(3)
+        turn_copy(4)
+        a_interleave(units[1])
+        turn_copy(5)
+        weigh_on_gpsimd(slot_steps(before_last)[:2])
+        gain(half_steps(last, 0))
+        weigh_on_vector(slot_steps(before_last)[2:])
+
+        descriptors(0, 0)
+        a_quantize(units[1])
+        traces_quantize(4)
+        descriptors(0, 1)
+        traces_quantize(5)
+        turn(6)
+        turn(7)
+        turn_copy(6)
+        turn_copy(7)
+        a_interleave(units[3], SHARE, BANK, on_scalar)
+        traces_quantize(6)
+        a_interleave(units[3], 0, SHARE)
+        descriptors(0, 2)
+        traces_quantize(7)
+        a_interleave(units[2])
+        descriptors(0, 3)
+        a_quantize(units[3])
+        sigmoid(half_steps(last, 0))
+
+        descriptors(1, 0)
+        z_quantize(0)
+        a_quantize(units[2])
+        a_interleave(before_last, 0, SHARE)
+        descriptors(1, 1)
+        z_quantize(1, *column_tiles[0])
+        weigh_on_vector(half_steps(last, 0))
+        descriptors(1, 2)
+        z_quantize(1, *column_tiles[1])
+        descriptors(1, 3)
+        a_interleave(before_last, SHARE, BANK, on_scalar)
+        z_quantize(1, *column_tiles[2])
+
+        for j in range(TILES):
+            out_pass(0, j, 0)
+        z_quantize(1, *column_tiles[3])
+        a_interleave(last, 0, HALF)
+        a_quantize(last, 0, HALF)
+        for j in range(TILES):
+            out_pass(0, j, 1)
+            out_store(0, j, on_vector if j == 1 else on_scalar)
+        a_quantize(before_last)
+
+        for step in half_steps(last, 1):
+            field([step])
+            gain_and_sigmoid([step])
+        out_tile(1, 0, on_vector)
+        weigh_on_vector(half_steps(last, 1))
+        for cols in column_tiles[TILES // 2 :]:
+            a_interleave(last, *cols)
+        for cols in column_tiles[TILES // 2 :]:
+            a_quantize(last, *cols)
+        for j in range(1, TILES):
+            out_tile(1, j, on_scalar)
+        for j in range(TILES):
+            out_tile(2, j, on_vector if j % 2 else on_scalar)

from contextlib import ExitStack

import concourse.mybir as mybir
from concourse.masks import make_identity

R, V, K, C = 1024, 1536, 2048, 512
FLOPS = 2 * R * V * V + 2 * R * K * C + 2 * R * V * C

F32 = mybir.dt.float32
BF16 = mybir.dt.bfloat16
I32 = mybir.dt.int32
U32 = mybir.dt.uint32
U8 = mybir.dt.uint8
FP8X4 = mybir.dt.float8_e4m3fn_x4
FP4X4 = mybir.dt.float4_e2m1fn_x4
ACT = mybir.ActivationFunctionType
ALU = mybir.AluOpType

P = 128
SLOTS = 4
RUN = 4
PASS = P * SLOTS
BANK = 512
HALF = BANK // 2
BANKS = 8
QUADS = 4
R_PASSES = R // PASS
V_PASSES = V // PASS
K_PASSES = K // PASS
V_CHUNKS = V // BANK
TILES = BANK // P

SHARE = 256
GPSIMD_SLOTS = 3

WIDE_BUFS = 3
PROB_BUFS = 8
A_ROWS_BUFS = 5
GROUPED_BUFS = 4
TURNED_BUFS = 4


def tile_qubo_replica_flips_s12_kernel(
    tc, states_words, states_scales, couplings_words, couplings_scales, flip, weight, traces, proj, out
):
    nc = tc.nc
    with ExitStack() as ctx:
        keep = ctx.enter_context(tc.tile_pool(name="keep", bufs=1))
        work = ctx.enter_context(tc.tile_pool(name="work", bufs=1))
        psum = ctx.enter_context(tc.psum_pool(name="psum", bufs=1))
        ctx.enter_context(tc.manual_schedule())

        banks_used = []

        def bank_tile(shape):
            tag = "bank%d" % (len(banks_used) % BANKS)
            banks_used.append(tag)
            return psum.tile(shape, F32, name=tag, tag=tag)

        def kept(name, shape, dtype):
            return keep.tile(shape, dtype, name=name, tag=name, align_bytes=64)

        def pooled(tag, bufs, shape, dtype):
            return work.tile(shape, dtype, name=tag, tag=tag, bufs=bufs, align_bytes=64)

        def mx_pair(name):
            return kept(name + "_codes", [P, BANK], U32), kept(name + "_scales", [P, BANK], U8)

        def grouped_tile(tag, bufs):
            return pooled(tag, bufs, [P, BANK, SLOTS], BF16)

        def quantize(pair, grouped, c0=0, c1=BANK):
            codes, scales = pair
            nc.vector.quantize_mx(
                out=codes[:, c0:c1].bitcast(FP8X4),
                scales=scales[:, c0:c1],
                in_=grouped[:, c0:c1, :].rearrange("p c t -> p (c t)"),
            )

        def interleave(copy, grouped, rows, c0, c1):
            copy(
                out=grouped[:, c0:c1, :].rearrange("p (c i) t -> p c t i", i=4),
                in_=rows[:, :, c0:c1].rearrange("p t (c i) -> p c t i", i=4),
            )

        units = [(c, g) for c in range(V_CHUNKS) for g in range(R_PASSES)]
        trace_passes = [(g, kp) for g in range(R_PASSES) for kp in range(K_PASSES)]
        column_tiles = [(j * P, (j + 1) * P) for j in range(TILES)]

        x_raw = [kept("x_raw%d" % g, [P, V_PASSES, PASS // 2], I32) for g in range(R_PASSES)]
        xs_raw = [kept("xs_raw%d" % g, [P, V_PASSES, PASS // 4], I32) for g in range(R_PASSES)]
        j_words = [kept("j_words%d" % c, [P, V_PASSES, 2 * BANK], U8) for c in range(V_CHUNKS)]
        js_first = kept("js_first", [P, V_PASSES, BANK], U8)
        js_rest = kept("js_rest", [P, V_PASSES, V - BANK], U8)
        proj_raw = [kept("proj_raw%d" % kp, [P, SLOTS, C], BF16) for kp in range(K_PASSES)]
        w_raw = kept("w_raw", [P, R_PASSES, RUN * SLOTS], BF16)
        ident = kept("ident", [P, P], F32)
        warm = kept("warm", [P, 1], F32)
        flip_sb = {}
        traces_raw = {}

        def load_x_words(g):
            src = states_words.bitcast(I32)[:, :, g * PASS // 2 : (g + 1) * PASS // 2]
            nc.sync.dma_start(out=x_raw[g][:], in_=src.rearrange("k p n -> p k n"))

        def load_j_words(c):
            src = couplings_words.bitcast(I32)[:, :, c * BANK // 2 : (c + 1) * BANK // 2]
            nc.sync.dma_start(out=j_words[c][:].bitcast(I32), in_=src.rearrange("k p n -> p k n"))

        def load_scale_rows(queue, plane, scales, n0, n1, quads):
            src = scales.bitcast(I32)[:, :, n0 // 4 : n1 // 4]
            for q in quads:
                queue.dma_start(
                    out=plane[32 * q : 32 * q + 4, :, :],
                    in_=src[:, 4 * q : 4 * q + 4, :].rearrange("k r n -> r k n"),
                )

        def load_flip(c, g):
            flip_sb[(c, g)] = kept("flip%d_%d" % (c, g), [P, SLOTS, BANK], BF16)
            src = flip[g * PASS : (g + 1) * PASS, c * BANK : (c + 1) * BANK]
            src = src.rearrange("(m t i) v -> i m t v", t=SLOTS, i=RUN)
            for i in range(RUN):
                nc.sync.dma_start(out=flip_sb[(c, g)][i:P:RUN, :, :], in_=src[i])

        def load_traces(piece, g, kp):
            width = piece.shape[2]
            src = traces[g * PASS : (g + 1) * PASS, kp * PASS : kp * PASS + width]
            nc.sync.dma_start(out=piece[:], in_=src.rearrange("(a i) k -> a i k", i=RUN))
            for j in range(width // PASS):
                traces_raw[(g, kp + j)] = (piece, j)

        def load_traces_pass(g, kp):
            load_traces(kept("traces%d_%d" % (g, kp), [P, RUN, PASS], BF16), g, kp)

        def load_traces_pair(g, kp):
            load_traces(pooled("wide", WIDE_BUFS, [P, RUN, 2 * PASS], BF16), g, kp)

        def load_proj(kp):
            src = proj[kp * PASS : (kp + 1) * PASS, :]
            nc.sync.dma_start(out=proj_raw[kp][:], in_=src.rearrange("(p t) c -> p t c", t=SLOTS))

        weight_span = RUN * (SLOTS - 1) + 1

        def load_weight():
            src = weight.rearrange("(g m x) -> m g x", g=R_PASSES, x=RUN * SLOTS)
            for i in range(RUN):
                nc.gpsimd.dma_start(out=w_raw[i:P:RUN, :, 0:weight_span], in_=src[:, :, i : i + weight_span])

        js_first_words = js_first[:].bitcast(I32)
        js_rest_words = js_rest[:].bitcast(I32)
        nc.vector.memset(js_first_words, 0)
        nc.vector.memset(xs_raw[0][:], 0)
        nc.vector.memset(warm[:], 0.0)
        nc.vector.memset(xs_raw[1][:], 0)
        nc.vector.memset(js_rest_words, 0)
        nc.scalar.activation(out=warm[:], in_=warm[:], func=ACT.Sigmoid)

        load_x_words(0)
        load_scale_rows(nc.sync, xs_raw[0], states_scales, 0, PASS, range(QUADS))
        load_j_words(0)
        load_scale_rows(nc.sync, js_first_words, couplings_scales, 0, BANK, range(QUADS // 2))
        load_scale_rows(nc.gpsimd, js_first_words, couplings_scales, 0, BANK, range(QUADS // 2, QUADS))
        make_identity(nc, ident[:])
        load_weight()
        load_flip(*units[0])
        load_x_words(1)
        load_scale_rows(nc.sync, xs_raw[1], states_scales, PASS, R, range(QUADS))
        load_proj(0)
        load_flip(*units[1])
        load_j_words(1)
        load_scale_rows(nc.sync, js_rest_words, couplings_scales, BANK, V, range(QUADS))
        load_proj(1)
        load_traces_pass(0, 0)
        load_flip(*units[2])
        load_proj(2)
        load_flip(*units[3])
        load_traces_pass(0, 1)
        load_j_words(2)
        load_proj(3)
        load_traces_pair(0, 2)
        load_flip(*units[4])
        load_traces_pair(1, 0)
        load_flip(*units[5])
        load_traces_pair(1, 2)

        x_codes = [kept("x_codes%d" % g, [P, SLOTS, V_PASSES, 2 * P], U8) for g in range(R_PASSES)]
        x_scales = [kept("x_scales%d" % g, [P, SLOTS, V_PASSES, P], U8) for g in range(R_PASSES)]
        proj_q = [mx_pair("proj_q%d" % kp) for kp in range(K_PASSES)]
        traces_q = {(g, kp): mx_pair("traces_q%d_%d" % (g, kp)) for g, kp in trace_passes}
        z_q = [mx_pair("z_q%d" % g) for g in range(R_PASSES)]
        a_q = {(c, g): mx_pair("a_q%d_%d" % (c, g)) for c, g in units}

        def order_states(g):
            nc.vector.tensor_copy(
                out=x_codes[g][:].bitcast(I32).rearrange("p t k (m h) -> p t (k m) h", h=2),
                in_=x_raw[g][:].rearrange("p k (m t h) -> p t (k m) h", t=SLOTS, h=2),
            )
            nc.vector.tensor_copy(
                out=x_scales[g][:].bitcast(I32).rearrange("p t k m -> p t (k m)"),
                in_=xs_raw[g][:].rearrange("p k (m t) -> p t (k m)", t=SLOTS),
            )

        def slot_steps(unit):
            return [(unit, t, 1, 0, BANK) for t in range(SLOTS)]

        def half_steps(unit, h):
            return [(unit, t, 2, h * HALF, HALF) for t in range(0, SLOTS, 2)]

        field_banks = {}
        prob = {}
        a_rows = {}
        a_grouped = {}

        def field(steps):
            for step in steps:
                (c, g), t0, slots, v0, width = step
                j_scales, s0 = (js_first, v0) if c == 0 else (js_rest, (c - 1) * BANK + v0)
                field_banks[step] = bank_tile([P, slots, width])
                for e in range(slots):
                    for k in range(V_PASSES):
                        nc.tensor.matmul_mx(
                            out=field_banks[step][:, e, :],
                            lhsT=x_codes[g][:, t0 + e, k, :].bitcast(FP4X4),
                            lhsT_scale=x_scales[g][:, t0 + e, k, :],
                            rhs=j_words[c][:, k, 2 * v0 : 2 * (v0 + width)].bitcast(FP4X4),
                            rhs_scale=j_scales[:, k, s0 : s0 + width],
                            start=(k == 0),
                            stop=(k == V_PASSES - 1),
                        )

        def gain(steps):
            for step in steps:
                unit, t0, slots, v0, width = step
                prob[step] = pooled("prob", PROB_BUFS, [P, slots, width], F32)
                nc.vector.tensor_tensor(
                    out=prob[step][:],
                    in0=field_banks[step][:],
                    in1=flip_sb[unit][:, t0 : t0 + slots, v0 : v0 + width],
                    op=ALU.mult,
                )

        def sigmoid(steps):
            for step in steps:
                nc.scalar.activation(out=prob[step][:], in_=prob[step][:], func=ACT.Sigmoid)

        def gain_and_sigmoid(steps):
            for step in steps:
                gain([step])
                sigmoid([step])

        def a_rows_tile(unit):
            if unit not in a_rows:
                a_rows[unit] = pooled("a_rows", A_ROWS_BUFS, [P, SLOTS, BANK], BF16)
            return a_rows[unit]

        def weigh_on_vector(steps):
            for step in steps:
                unit, t0, slots, v0, width = step
                for e in range(slots):
                    t = t0 + e
                    nc.vector.tensor_scalar(
                        out=a_rows_tile(unit)[:, t, v0 : v0 + width],
                        in0=prob[step][:, e, :],
                        scalar1=w_raw[:, unit[1], RUN * t : RUN * t + 1],
                        scalar2=None,
                        op0=ALU.mult,
                    )

        def weigh_on_gpsimd(steps):
            unit = steps[0][0]
            w_col = kept("w_col%d_%d" % unit, [P, SLOTS], F32)
            nc.vector.tensor_copy(out=w_col[:], in_=w_raw[:, unit[1], 0:weight_span:RUN])
            for step in steps:
                t = step[1]
                nc.gpsimd.tensor_scalar(
                    out=a_rows_tile(unit)[:, t, :],
                    in0=prob[step][:, 0, :],
                    scalar1=w_col[:, t : t + 1],
                    scalar2=0.0,
                    op0=ALU.mult,
                    op1=ALU.add,
                )

        def a_interleave(unit, c0=0, c1=BANK, copy=nc.vector.tensor_copy):
            if unit not in a_grouped:
                a_grouped[unit] = grouped_tile("grouped", GROUPED_BUFS)
            interleave(copy, a_grouped[unit], a_rows[unit], c0, c1)

        def a_quantize(unit, c0=0, c1=BANK):
            quantize(a_q[unit], a_grouped[unit], c0, c1)

        turn_banks = {}
        turned = {}
        proj_grouped = {}
        z_grouped = {}

        def turn(n):
            piece, j = traces_raw[trace_passes[n]]
            words = piece[:].bitcast(F32)
            w0 = j * (PASS // 2)
            for e in range(2):
                turn_banks[(n, e)] = bank_tile([P, 2, 2, P])
                for x in range(2):
                    for u in range(2):
                        nc.tensor.transpose(
                            turn_banks[(n, e)][:, x, u, :], words[:, 2 * e + x, w0 + u : w0 + PASS // 2 : 2], ident[:]
                        )

        def turn_copy(n):
            turned[n] = grouped_tile("turned", TURNED_BUFS)
            dst = turned[n][:].rearrange("p c t -> p (c t)").bitcast(F32)
            for e in range(2):
                nc.scalar.copy(
                    out=dst.rearrange("p (t m e w) -> p e m t w", t=SLOTS, e=2, w=4)[:, e],
                    in_=turn_banks[(n, e)][:].rearrange("p x u (m t) -> p m t (x u)", t=SLOTS),
                )

        def traces_quantize(n):
            quantize(traces_q[trace_passes[n]], turned[n])

        def proj_interleave(kp):
            proj_grouped[kp] = grouped_tile("grouped", GROUPED_BUFS)
            interleave(nc.vector.tensor_copy, proj_grouped[kp], proj_raw[kp], 0, SHARE)
            interleave(nc.scalar.copy, proj_grouped[kp], proj_raw[kp], SHARE, C)

        def proj_quantize(kp):
            quantize(proj_q[kp], proj_grouped[kp])

        def descriptors(g, j):
            if j == 0:
                z_grouped[g] = grouped_tile("z_grouped", R_PASSES)
            cols = slice(*column_tiles[j])
            bank = bank_tile([P, SLOTS, P])
            for t in range(SLOTS):
                replicas = slice(t * P, (t + 1) * P)
                for kp in range(K_PASSES):
                    nc.tensor.matmul_mx(
                        out=bank[:, t, :],
                        lhsT=traces_q[(g, kp)][0][:, replicas].bitcast(FP8X4),
                        lhsT_scale=traces_q[(g, kp)][1][:, replicas],
                        rhs=proj_q[kp][0][:, cols].bitcast(FP8X4),
                        rhs_scale=proj_q[kp][1][:, cols],
                        start=(kp == 0),
                        stop=(kp == K_PASSES - 1),
                    )
            nc.scalar.copy(out=z_grouped[g][:, cols, :], in_=bank[:].rearrange("p t c -> p c t"))

        def z_quantize(g, c0=0, c1=C):
            quantize(z_q[g], z_grouped[g], c0, c1)

        out_banks = {}
        results = {}

        def out_pass(c, j, g):
            cols = slice(*column_tiles[j])
            if g == 0:
                out_banks[(c, j)] = bank_tile([P, C])
            nc.tensor.matmul_mx(
                out=out_banks[(c, j)][:],
                lhsT=a_q[(c, g)][0][:, cols].bitcast(FP8X4),
                lhsT_scale=a_q[(c, g)][1][:, cols],
                rhs=z_q[g][0][:].bitcast(FP8X4),
                rhs_scale=z_q[g][1][:],
                start=(g == 0),
                stop=(g == R_PASSES - 1),
            )

        def out_store(c, j, copy):
            if j == 0:
                results[c] = pooled("wide", WIDE_BUFS, [P, TILES, C], F32)
            copy(out=results[c][:, j, :], in_=out_banks[(c, j)][:])
            nc.sync.dma_start(out=out[c * BANK + j * P : c * BANK + (j + 1) * P, :], in_=results[c][:, j, :])

        def out_tile(c, j, copy):
            for g in range(R_PASSES):
                out_pass(c, j, g)
            out_store(c, j, copy)

        on_vector, on_scalar = nc.vector.tensor_copy, nc.scalar.copy
        last = units[-1]
        before_last = units[-2]

        order_states(0)
        field(slot_steps(units[0]))
        gain_and_sigmoid(slot_steps(units[0])[:2])
        order_states(1)
        gain_and_sigmoid(slot_steps(units[0])[2:])

        for n in range(1, len(units) - 1):
            unit, previous = units[n], units[n - 1]
            closing = unit == before_last
            if n >= 3:
                turn_copy(n - 3)
            proj_interleave(n - 1)
            if closing:
                traces_quantize(0)
            if n >= 2:
                proj_quantize(n - 2)
            if closing:
                traces_quantize(1)
            if n == 2:
                a_interleave(units[0])
            if n == 3:
                a_quantize(units[0])
            field(slot_steps(unit))
            if n >= 2:
                turn(n - 2)
            weigh_on_gpsimd(slot_steps(previous)[:GPSIMD_SLOTS])
            if closing:
                gain(slot_steps(unit))
            else:
                gain_and_sigmoid(slot_steps(unit))
            weigh_on_vector(slot_steps(previous)[GPSIMD_SLOTS:])

        turn(3)
        turn_copy(2)
        proj_quantize(K_PASSES - 1)
        turn_copy(3)
        sigmoid(slot_steps(before_last))
        field(half_steps(last, 0))
        traces_quantize(2)
        turn(4)
        turn(5)
        traces_quantize(3)
        turn_copy(4)
        a_interleave(units[1])
        turn_copy(5)
        weigh_on_gpsimd(slot_steps(before_last)[:2])
        gain(half_steps(last, 0))
        weigh_on_vector(slot_steps(before_last)[2:])

        descriptors(0, 0)
        a_quantize(units[1])
        traces_quantize(4)
        descriptors(0, 1)
        traces_quantize(5)
        turn(6)
        turn(7)
        turn_copy(6)
        turn_copy(7)
        a_interleave(units[3], SHARE, BANK, on_scalar)
        traces_quantize(6)
        a_interleave(units[3], 0, SHARE)
        descriptors(0, 2)
        traces_quantize(7)
        a_interleave(units[2])
        descriptors(0, 3)
        a_quantize(units[3])
        sigmoid(half_steps(last, 0))

        descriptors(1, 0)
        z_quantize(0)
        a_quantize(units[2])
        a_interleave(before_last, 0, SHARE)
        descriptors(1, 1)
        z_quantize(1, *column_tiles[0])
        weigh_on_vector(half_steps(last, 0))
        descriptors(1, 2)
        z_quantize(1, *column_tiles[1])
        descriptors(1, 3)
        a_interleave(before_last, SHARE, BANK, on_scalar)
        z_quantize(1, *column_tiles[2])

        for j in range(TILES):
            out_pass(0, j, 0)
        z_quantize(1, *column_tiles[3])
        a_interleave(last, 0, HALF)
        a_quantize(last, 0, HALF)
        for j in range(TILES):
            out_pass(0, j, 1)
            out_store(0, j, on_vector if j == 1 else on_scalar)
        a_quantize(before_last)

        for step in half_steps(last, 1):
            field([step])
            gain_and_sigmoid([step])
        out_tile(1, 0, on_vector)
        weigh_on_vector(half_steps(last, 1))
        for cols in column_tiles[TILES // 2 :]:
            a_interleave(last, *cols)
        for cols in column_tiles[TILES // 2 :]:
            a_quantize(last, *cols)
        for j in range(1, TILES):
            out_tile(1, j, on_scalar)
        for j in range(TILES):
            out_tile(2, j, on_vector if j % 2 else on_scalar)
